import numpy as np
import ml_dtypes


def mxq(x, axis, fmt="e4m3"):
    dtype, down = {"e4m3": (ml_dtypes.float8_e4m3fn, 7), "e5m2": (ml_dtypes.float8_e5m2, 14)}[fmt]
    v = np.moveaxis(np.asarray(x, np.float32).astype(ml_dtypes.bfloat16).astype(np.float64), axis, -1)
    blocks = v.reshape(v.shape[:-1] + (-1, 32))
    amax = np.abs(blocks).max(-1, keepdims=True)
    byte = np.maximum(np.where(amax > 0, np.frexp(amax)[1] - 1 + 127, 0) - down, 1)
    scale = np.exp2(byte - 127.0)
    codes = (blocks / scale).astype(np.float32).astype(dtype).astype(np.float64)
    return np.moveaxis((codes * scale).reshape(v.shape), -1, axis)


WIDE = False


def mx_kscale(k):
    if not WIDE:
        return np.ones(k)
    levels = np.array([10, -10, 5, -5, 0])
    if k % 512:
        return np.exp2(np.random.permutation(np.resize(levels, k // 32))).repeat(32)
    a = np.empty((k // 512, 16))
    for p in range(k // 512):
        a[p, :8] = np.random.permutation(np.resize(levels, 8))
        for g in range(8):
            far = levels[np.abs(levels - a[p, g]) >= 10]
            a[p, g + 8] = far[np.random.randint(len(far))]
    return np.exp2(a.ravel()).repeat(32)


def f64(x):
    return np.asarray(x).astype(np.float64)


def striped8(idx):
    return np.concatenate([x.reshape(-1, 16).T for x in idx]).astype(np.uint16)


def runs(offs, k):
    lists = np.stack([offs[16 * r : 16 * r + 16].T.reshape(-1) for r in range(8)]).astype(np.int64)
    return lists[np.arange(k) % 512 // 64]


def pack_weight(w):
    k, n = w.shape
    w = f64(np.asarray(w, np.float32).astype(ml_dtypes.bfloat16)).reshape(k // 32, 32, n)
    amax = np.abs(w).max(1)
    byte = np.clip(np.where(amax > 0, np.frexp(amax)[1] - 1 + 127 - 7, 1), 1, 254)
    scaled = (w * np.exp2(127.0 - byte)[:, None, :]).reshape(k, n).astype(np.float32)
    words = np.ascontiguousarray(scaled.reshape(k // 512, 128, 4, n).transpose(0, 1, 3, 2)).astype(ml_dtypes.float8_e4m3fn).view(np.uint8)
    return words, np.ascontiguousarray(byte.astype(np.uint8).reshape(k // 512, 16, n))


def unpack_weight(words, scales):
    g, p, n, _ = words.shape
    vals = np.ascontiguousarray(words).view(ml_dtypes.float8_e4m3fn).astype(np.float64) * np.repeat(np.exp2(scales.astype(np.float64) - 127.0), 8, axis=1)[..., None]
    return vals.transpose(0, 1, 3, 2).reshape(g * 512, n)


K, T, S, H, N, V = 1024, 2048, 1024, 512, 256, 512


def setup_inputs():
    n = np.random.standard_normal
    s = mx_kscale(K)[:, None]
    u = mx_kscale(H)
    packed_xT = pack_weight(n((K, T)) * s)
    packed_w2 = pack_weight(n((H, N)) / np.sqrt(H) / u[:, None])
    return {
        "x_words": packed_xT[0],
        "x_scales": packed_xT[1],
        "w1": (n((K, H)) / np.sqrt(K) / s * u).astype(np.float32),
        "w2_words": packed_w2[0],
        "w2_scales": packed_w2[1],
        "offs": striped8(np.stack([np.random.permutation(T)[:S] for _ in range(8)])),
    }


def reference(x_words, x_scales, w1, w2_words, w2_scales, offs):
    xq = unpack_weight(x_words, x_scales)[np.arange(K)[:, None], runs(offs, K)]
    y = mxq(f64(w1), 0, "e4m3").T @ xq
    z = np.maximum(y[:, :V], y[:, V:2 * V])
    return unpack_weight(w2_words, w2_scales).T @ mxq(z, 0, "e4m3")

@@ -1,0 +1,190 @@
+from contextlib import ExitStack
+
+import concourse.mybir as mybir
+from concourse.masks import make_identity
+
+K, T, S, H, N, V = 1024, 2048, 1024, 512, 256, 512
+FLOPS = 2 * K * H * S + 2 * H * N * V
+
+F32 = mybir.dt.float32
+BF16 = mybir.dt.bfloat16
+I32 = mybir.dt.int32
+U32 = mybir.dt.uint32
+U16 = mybir.dt.uint16
+U8 = mybir.dt.uint8
+FP8X4 = mybir.dt.float8_e4m3fn_x4
+
+P = 128
+PACK = 4
+K_PASS = P * PACK
+PASSES = K // K_PASS
+QUADRANT = 32
+SLICE = 256
+CHUNK = 128
+CHUNKS = V // CHUNK
+SCALAR_COLS = 256
+
+
+def tile_picked_phpool_none_p_kernel(tc, x_words, x_scales, w1, w2_words, w2_scales, offs, out):
+    nc = tc.nc
+    with ExitStack() as ctx:
+        keep = ctx.enter_context(tc.tile_pool(name="keep", bufs=1))
+        reuse = ctx.enter_context(tc.tile_pool(name="reuse", bufs=1))
+        psum = ctx.enter_context(tc.psum_pool(name="psum", bufs=1))
+
+        offsets = keep.tile([P, S // 16], U16, name="offsets")
+        nc.sync.dma_start(offsets[:], offs)
+
+        scale_table = keep.tile([P, T], U8, name="scale_table", tag="late_words", align_bytes=64)
+        nc.vector.memset(scale_table[:].bitcast(I32), 0)
+        nc.scalar.dma_start(
+            out=scale_table[0:P:4, :].bitcast(I32),
+            in_=x_scales.rearrange("z q c -> q z c").bitcast(I32),
+        )
+
+        x_planes = keep.tile([P, PASSES, S], U8, name="x_planes", align_bytes=64)
+        nc.vector.memset(x_planes[:].rearrange("p z s -> p (z s)").bitcast(I32), 0)
+
+        identity = keep.tile([P, P], F32, name="identity", align_bytes=64)
+        make_identity(nc, identity[:])
+
+        def load_words(z, table):
+            nc.sync.dma_start(
+                out=table[:].bitcast(I32),
+                in_=x_words[z].rearrange("p n t -> p (n t)").bitcast(I32),
+            )
+
+        def load_w1(z, raw):
+            nc.sync.dma_start(
+                out=raw[:],
+                in_=w1[z * K_PASS : (z + 1) * K_PASS, :].rearrange("(p j) c -> p j c", j=PACK),
+            )
+
+        raw0 = keep.tile([P, PACK, H], F32, name="raw0", tag="late_w2", align_bytes=64)
+        load_w1(0, raw0)
+        table0 = keep.tile([P, T], U32, name="table0", align_bytes=64)
+        load_words(0, table0)
+        raw1 = keep.tile([P, PACK, H], F32, name="raw1", align_bytes=64)
+        load_w1(1, raw1)
+        w1_raw = [raw0, raw1]
+
+        picked_scales = keep.tile([P, S], U8, name="picked_scales", tag="late_plane", align_bytes=64)
+        nc.vector.tensor_copy(picked_scales[:], scale_table[:].indirect(offsets[:]))
+        for q in range(4):
+            nc.scalar.dma_start(
+                out=x_planes[QUADRANT * q : QUADRANT * q + 4, :, :].bitcast(I32),
+                in_=picked_scales[QUADRANT * q : QUADRANT * (q + 1) : 4, :].bitcast(I32),
+            )
+
+        table1 = keep.tile([P, T], U32, name="table1", tag="late_words", align_bytes=64)
+        load_words(1, table1)
+        word_table = [table0, table1]
+
+        w2_plane = keep.tile([P, N], U8, name="w2_plane", tag="late_plane", align_bytes=64)
+        nc.gpsimd.memset(w2_plane[:].bitcast(I32), 0)
+        for q in range(4):
+            nc.sync.dma_start(
+                out=w2_plane[QUADRANT * q : QUADRANT * q + 4, :].bitcast(I32),
+                in_=w2_scales[0, 4 * q : 4 * q + 4, :].bitcast(I32),
+            )
+
+        w1_codes = [keep.tile([P, H], U32, name="w1_codes%d" % z, align_bytes=64) for z in range(PASSES)]
+        w1_plane = [keep.tile([P, H], U8, name="w1_plane%d" % z, align_bytes=64) for z in range(PASSES)]
+
+        def quantize_w1(z):
+            grouped = reuse.tile([P, H, PACK], BF16, name="w1_grouped%d" % z, align_bytes=64, offset=4096 * z)
+            a, b = slice(0, SCALAR_COLS), slice(SCALAR_COLS, H)
+            nc.scalar.copy(
+                out=grouped[:, a, :].rearrange("p (c i) j -> p c j i", i=4),
+                in_=w1_raw[z][:, :, a].rearrange("p j (c i) -> p c j i", i=4),
+            )
+            nc.vector.tensor_copy(
+                out=grouped[:, b, :].rearrange("p (c i) j -> p c j i", i=4),
+                in_=w1_raw[z][:, :, b].rearrange("p j (c i) -> p c j i", i=4),
+            )
+            nc.vector.quantize_mx(
+                out=w1_codes[z][:].bitcast(FP8X4),
+                scales=w1_plane[z][:],
+                in_=grouped[:].rearrange("p c j -> p (c j)"),
+            )
+
+        banks = [psum.tile([P, H], F32, name="bank%d" % b, tag="bank%d" % b) for b in range(2 * CHUNKS)]
+        starts = [V, 0, V + SLICE, SLICE]
+
+        def gather(z, s0, offset):
+            picked = reuse.tile([P, SLICE], U32, name="picked%d_%d" % (z, s0), align_bytes=64, offset=offset)
+            nc.vector.tensor_copy(picked[:], word_table[z][:].indirect(offsets[:, s0 // 16 : (s0 + SLICE) // 16]))
+            return picked
+
+        def project(z, s0, picked):
+            for c0 in range(0, SLICE, CHUNK):
+                nc.tensor.matmul_mx(
+                    out=banks[(s0 + c0) // CHUNK][:],
+                    lhsT=picked[:, c0 : c0 + CHUNK].bitcast(FP8X4),
+                    lhsT_scale=x_planes[:, z, s0 + c0 : s0 + c0 + CHUNK],
+                    rhs=w1_codes[z][:].bitcast(FP8X4),
+                    rhs_scale=w1_plane[z][:],
+                    start=(z == 0),
+                    stop=(z == PASSES - 1),
+                )
+
+        first = [gather(0, s0, 8192 + 1024 * i) for i, s0 in enumerate(starts[:2])]
+        quantize_w1(0)
+        first = first + [gather(0, s0, 1024 * i) for i, s0 in enumerate(starts[2:])]
+        w2_codes = keep.tile([P, N], U32, name="w2_codes", tag="late_w2", align_bytes=64)
+        nc.sync.dma_start(
+            out=w2_codes[:].bitcast(I32),
+            in_=w2_words[0].rearrange("p n t -> p (n t)").bitcast(I32),
+        )
+        for s0, picked in zip(starts, first):
+            project(0, s0, picked)
+        quantize_w1(1)
+        for i, s0 in enumerate(starts):
+            project(1, s0, gather(1, s0, 4096 + 1024 * i))
+
+        order = "v (p u e) -> v u p e"
+        split = "v (u p e) -> v u p e"
+        seconds = []
+        for c in range(CHUNKS):
+            second = keep.tile([P, H], F32, name="second%d" % c, align_bytes=64)
+            nc.scalar.copy(
+                out=second[:].rearrange(split, u=2, e=2),
+                in_=banks[CHUNKS + c][:].rearrange(order, u=2, e=2),
+            )
+            seconds.append(second)
+
+        out_view = out.rearrange("(h p) v -> p h v", p=P)
+        for c in range(CHUNKS):
+            z_rows = keep.tile([P, H], BF16, name="z_rows%d" % c, align_bytes=64)
+            nc.vector.tensor_tensor(
+                out=z_rows[:].rearrange(split, u=2, e=2),
+                in0=banks[c][:].rearrange(order, u=2, e=2),
+                in1=seconds[c][:].rearrange(split, u=2, e=2),
+                op=mybir.AluOpType.max,
+            )
+            pairs = z_rows[:].bitcast(F32)
+            turned = psum.tile([P, 2, CHUNK], F32, name="turned%d" % c, tag="bank%d" % (CHUNKS + c))
+            for u in range(2):
+                nc.tensor.transpose(turned[:, u, :], pairs[:, u * P : (u + 1) * P], identity[:])
+            z_grouped = keep.tile([P, CHUNK * PACK], BF16, name="z_grouped%d" % c, align_bytes=64)
+            nc.scalar.copy(
+                out=z_grouped[:].bitcast(F32).rearrange("p (v u) -> p v u", u=2),
+                in_=turned[:].rearrange("p u v -> p v u"),
+            )
+            z_codes = keep.tile([P, CHUNK], U32, name="z_codes%d" % c, align_bytes=64)
+            z_plane = keep.tile([P, CHUNK], U8, name="z_plane%d" % c, align_bytes=64)
+            nc.vector.quantize_mx(out=z_codes[:].bitcast(FP8X4), scales=z_plane[:], in_=z_grouped[:])
+            acc = psum.tile([P, N // P, CHUNK], F32, name="acc%d" % c, tag="bank%d" % c)
+            for h in range(N // P):
+                nc.tensor.matmul_mx(
+                    out=acc[:, h, :],
+                    lhsT=w2_codes[:, h * P : (h + 1) * P].bitcast(FP8X4),
+                    lhsT_scale=w2_plane[:, h * P : (h + 1) * P],
+                    rhs=z_codes[:].bitcast(FP8X4),
+                    rhs_scale=z_plane[:],
+                    start=True,
+                    stop=True,
+                )
+            result = keep.tile([P, N // P, CHUNK], F32, name="result%d" % c, align_bytes=64)
+            nc.scalar.copy(out=result[:], in_=acc[:])
+            nc.sync.dma_start(out=out_view[:, :, c * CHUNK : (c + 1) * CHUNK], in_=result[:])

@@ -22,7 +22,7 @@ QUADRANT = 32
 SLICE = 256
 CHUNK = 128
 CHUNKS = V // CHUNK
-SCALAR_COLS = 256
+SCALAR_COLS = 320
 
 
 def tile_picked_phpool_none_p_kernel(tc, x_words, x_scales, w1, w2_words, w2_scales, offs, out):
@@ -30,6 +30,7 @@ def tile_picked_phpool_none_p_kernel(tc, x_words, x_scales, w1, w2_words, w2_sca
     with ExitStack() as ctx:
         keep = ctx.enter_context(tc.tile_pool(name="keep", bufs=1))
         reuse = ctx.enter_context(tc.tile_pool(name="reuse", bufs=1))
+        tail = ctx.enter_context(tc.tile_pool(name="tail", bufs=1))
         psum = ctx.enter_context(tc.psum_pool(name="psum", bufs=1))
 
         offsets = keep.tile([P, S // 16], U16, name="offsets")
@@ -37,7 +38,7 @@ def tile_picked_phpool_none_p_kernel(tc, x_words, x_scales, w1, w2_words, w2_sca
 
         scale_table = keep.tile([P, T], U8, name="scale_table", tag="late_words", align_bytes=64)
         nc.vector.memset(scale_table[:].bitcast(I32), 0)
-        nc.scalar.dma_start(
+        nc.sync.dma_start(
             out=scale_table[0:P:4, :].bitcast(I32),
             in_=x_scales.rearrange("z q c -> q z c").bitcast(I32),
         )
@@ -45,8 +46,10 @@ def tile_picked_phpool_none_p_kernel(tc, x_words, x_scales, w1, w2_words, w2_sca
         x_planes = keep.tile([P, PASSES, S], U8, name="x_planes", align_bytes=64)
         nc.vector.memset(x_planes[:].rearrange("p z s -> p (z s)").bitcast(I32), 0)
 
+        draft = reuse.tile([P, 1312], F32, name="draft", align_bytes=64, offset=8192 - 64)
+        make_identity(nc, draft[:, 0:P])
         identity = keep.tile([P, P], F32, name="identity", align_bytes=64)
-        make_identity(nc, identity[:])
+        nc.scalar.copy(identity[:], draft[:, 0:P])
 
         def load_words(z, table):
             nc.sync.dma_start(
@@ -62,16 +65,16 @@ def tile_picked_phpool_none_p_kernel(tc, x_words, x_scales, w1, w2_words, w2_sca
 
         raw0 = keep.tile([P, PACK, H], F32, name="raw0", tag="late_w2", align_bytes=64)
         load_w1(0, raw0)
-        table0 = keep.tile([P, T], U32, name="table0", align_bytes=64)
+        table0 = reuse.tile([P, T], U32, name="table0", align_bytes=64, offset=0)
         load_words(0, table0)
-        raw1 = keep.tile([P, PACK, H], F32, name="raw1", align_bytes=64)
+        raw1 = reuse.tile([P, PACK, H], F32, name="raw1", align_bytes=64, offset=13312)
         load_w1(1, raw1)
         w1_raw = [raw0, raw1]
 
-        picked_scales = keep.tile([P, S], U8, name="picked_scales", tag="late_plane", align_bytes=64)
+        picked_scales = reuse.tile([P, S], U8, name="picked_scales", align_bytes=64, offset=8192)
         nc.vector.tensor_copy(picked_scales[:], scale_table[:].indirect(offsets[:]))
         for q in range(4):
-            nc.scalar.dma_start(
+            nc.sync.dma_start(
                 out=x_planes[QUADRANT * q : QUADRANT * q + 4, :, :].bitcast(I32),
                 in_=picked_scales[QUADRANT * q : QUADRANT * (q + 1) : 4, :].bitcast(I32),
             )
@@ -80,7 +83,7 @@ def tile_picked_phpool_none_p_kernel(tc, x_words, x_scales, w1, w2_words, w2_sca
         load_words(1, table1)
         word_table = [table0, table1]
 
-        w2_plane = keep.tile([P, N], U8, name="w2_plane", tag="late_plane", align_bytes=64)
+        w2_plane = reuse.tile([P, N], U8, name="w2_plane", align_bytes=64, offset=8192)
         nc.gpsimd.memset(w2_plane[:].bitcast(I32), 0)
         for q in range(4):
             nc.sync.dma_start(
@@ -92,13 +95,14 @@ def tile_picked_phpool_none_p_kernel(tc, x_words, x_scales, w1, w2_words, w2_sca
         w1_plane = [keep.tile([P, H], U8, name="w1_plane%d" % z, align_bytes=64) for z in range(PASSES)]
 
         def quantize_w1(z):
-            grouped = reuse.tile([P, H, PACK], BF16, name="w1_grouped%d" % z, align_bytes=64, offset=4096 * z)
+            grouped = reuse.tile([P, H, PACK], BF16, name="w1_grouped%d" % z, align_bytes=64, offset=(9216, 21504)[z])
             a, b = slice(0, SCALAR_COLS), slice(SCALAR_COLS, H)
             nc.scalar.copy(
                 out=grouped[:, a, :].rearrange("p (c i) j -> p c j i", i=4),
                 in_=w1_raw[z][:, :, a].rearrange("p j (c i) -> p c j i", i=4),
             )
-            nc.vector.tensor_copy(
+            second_copy = nc.scalar.copy if z == 0 else nc.vector.tensor_copy
+            second_copy(
                 out=grouped[:, b, :].rearrange("p (c i) j -> p c j i", i=4),
                 in_=w1_raw[z][:, :, b].rearrange("p j (c i) -> p c j i", i=4),
             )
@@ -128,9 +132,9 @@ def tile_picked_phpool_none_p_kernel(tc, x_words, x_scales, w1, w2_words, w2_sca
                     stop=(z == PASSES - 1),
                 )
 
-        first = [gather(0, s0, 8192 + 1024 * i) for i, s0 in enumerate(starts[:2])]
+        first = [gather(0, s0, 25600 + 1024 * i) for i, s0 in enumerate(starts[:2])]
         quantize_w1(0)
-        first = first + [gather(0, s0, 1024 * i) for i, s0 in enumerate(starts[2:])]
+        first = first + [gather(0, s0, 9216 + 1024 * i) for i, s0 in enumerate(starts[2:])]
         w2_codes = keep.tile([P, N], U32, name="w2_codes", tag="late_w2", align_bytes=64)
         nc.sync.dma_start(
             out=w2_codes[:].bitcast(I32),
@@ -140,51 +144,81 @@ def tile_picked_phpool_none_p_kernel(tc, x_words, x_scales, w1, w2_words, w2_sca
             project(0, s0, picked)
         quantize_w1(1)
         for i, s0 in enumerate(starts):
-            project(1, s0, gather(1, s0, 4096 + 1024 * i))
+            project(1, s0, gather(1, s0, 21504 + 1024 * i))
 
         order = "v (p u e) -> v u p e"
         split = "v (u p e) -> v u p e"
         seconds = []
         for c in range(CHUNKS):
-            second = keep.tile([P, H], F32, name="second%d" % c, align_bytes=64)
+            second = tail.tile([P, H], F32, name="second%d" % c, align_bytes=64, offset=2048 * c)
             nc.scalar.copy(
                 out=second[:].rearrange(split, u=2, e=2),
                 in_=banks[CHUNKS + c][:].rearrange(order, u=2, e=2),
             )
             seconds.append(second)
 
-        out_view = out.rearrange("(h p) v -> p h v", p=P)
-        for c in range(CHUNKS):
-            z_rows = keep.tile([P, H], BF16, name="z_rows%d" % c, align_bytes=64)
-            nc.vector.tensor_tensor(
-                out=z_rows[:].rearrange(split, u=2, e=2),
-                in0=banks[c][:].rearrange(order, u=2, e=2),
-                in1=seconds[c][:].rearrange(split, u=2, e=2),
-                op=mybir.AluOpType.max,
-            )
-            pairs = z_rows[:].bitcast(F32)
-            turned = psum.tile([P, 2, CHUNK], F32, name="turned%d" % c, tag="bank%d" % (CHUNKS + c))
-            for u in range(2):
-                nc.tensor.transpose(turned[:, u, :], pairs[:, u * P : (u + 1) * P], identity[:])
-            z_grouped = keep.tile([P, CHUNK * PACK], BF16, name="z_grouped%d" % c, align_bytes=64)
-            nc.scalar.copy(
-                out=z_grouped[:].bitcast(F32).rearrange("p (v u) -> p v u", u=2),
-                in_=turned[:].rearrange("p u v -> p v u"),
-            )
-            z_codes = keep.tile([P, CHUNK], U32, name="z_codes%d" % c, align_bytes=64)
-            z_plane = keep.tile([P, CHUNK], U8, name="z_plane%d" % c, align_bytes=64)
-            nc.vector.quantize_mx(out=z_codes[:].bitcast(FP8X4), scales=z_plane[:], in_=z_grouped[:])
-            acc = psum.tile([P, N // P, CHUNK], F32, name="acc%d" % c, tag="bank%d" % c)
-            for h in range(N // P):
-                nc.tensor.matmul_mx(
-                    out=acc[:, h, :],
-                    lhsT=w2_codes[:, h * P : (h + 1) * P].bitcast(FP8X4),
-                    lhsT_scale=w2_plane[:, h * P : (h + 1) * P],
-                    rhs=z_codes[:].bitcast(FP8X4),
-                    rhs_scale=z_plane[:],
-                    start=True,
-                    stop=True,
+        groups = [(0, 2), (2, 3), (3, 4)]
+        z_grouped = [
+            keep.tile([P, (c1 - c0) * CHUNK * PACK], BF16, name="z_grouped%d" % c0, align_bytes=64)
+            for c0, c1 in groups
+        ]
+        for g, (c0, c1) in enumerate(groups):
+            for c in range(c0, c1):
+                z_rows = keep.tile([P, H], BF16, name="z_rows%d" % c, align_bytes=64)
+                nc.vector.tensor_tensor(
+                    out=z_rows[:].rearrange(split, u=2, e=2),
+                    in0=banks[c][:].rearrange(order, u=2, e=2),
+                    in1=seconds[c][:].rearrange(split, u=2, e=2),
+                    op=mybir.AluOpType.max,
                 )
-            result = keep.tile([P, N // P, CHUNK], F32, name="result%d" % c, align_bytes=64)
-            nc.scalar.copy(out=result[:], in_=acc[:])
-            nc.sync.dma_start(out=out_view[:, :, c * CHUNK : (c + 1) * CHUNK], in_=result[:])
+                pairs = z_rows[:].bitcast(F32)
+                turned = psum.tile([P, 2, CHUNK], F32, name="turned%d" % c, tag="bank%d" % (CHUNKS + c))
+                for u in range(2):
+                    nc.tensor.transpose(turned[:, u, :], pairs[:, u * P : (u + 1) * P], identity[:])
+                words = z_grouped[g][:].bitcast(F32)[:, (c - c0) * 2 * CHUNK : (c - c0 + 1) * 2 * CHUNK]
+                nc.scalar.copy(
+                    out=words.rearrange("p (v u) -> p v u", u=2),
+                    in_=turned[:].rearrange("p u v -> p v u"),
+                )
+
+        def second_layer(acc, h, z_codes, z_plane):
+            nc.tensor.matmul_mx(
+                out=acc,
+                lhsT=w2_codes[:, h * P : (h + 1) * P].bitcast(FP8X4),
+                lhsT_scale=w2_plane[:, h * P : (h + 1) * P],
+                rhs=z_codes[:].bitcast(FP8X4),
+                rhs_scale=z_plane[:],
+                start=True,
+                stop=True,
+            )
+
+        out_view = out.rearrange("(h p) v -> p h v", p=P)
+        for g, (c0, c1) in enumerate(groups):
+            width = (c1 - c0) * CHUNK
+            cols = slice(c0 * CHUNK, c1 * CHUNK)
+            z_codes = tail.tile(
+                [P, width], U32, name="z_codes%d" % g, align_bytes=64, offset=2048 * (CHUNKS - 1) + 4 * c0 * CHUNK
+            )
+            z_plane = keep.tile([P, width], U8, name="z_plane%d" % g, align_bytes=64)
+            nc.vector.quantize_mx(out=z_codes[:].bitcast(FP8X4), scales=z_plane[:], in_=z_grouped[g][:])
+            if g < len(groups) - 1:
+                acc = psum.tile([P, N // P, width], F32, name="acc%d" % g, tag="bank%d" % g)
+                for h in range(N // P):
+                    second_layer(acc[:, h, :], h, z_codes, z_plane)
+                result = keep.tile([P, N // P, width], F32, name="result%d" % g, align_bytes=64)
+                if g == 0:
+                    nc.scalar.copy(out=result[:], in_=acc[:])
+                else:
+                    nc.vector.tensor_copy(out=result[:], in_=acc[:])
+                nc.sync.dma_start(out=out_view[:, :, cols], in_=result[:])
+            else:
+                for h in range(N // P):
+                    acc = psum.tile([P, width], F32, name="acc_last%d" % h, tag="bank%d" % (g + h))
+                    second_layer(acc[:], h, z_codes, z_plane)
+                    result = keep.tile([P, width], F32, name="result_last%d" % h, align_bytes=64)
+                    if h == 0:
+                        nc.scalar.copy(out=result[:], in_=acc[:])
+                        nc.scalar.dma_start(out=out_view[:, h, cols], in_=result[:])
+                    else:
+                        nc.vector.tensor_copy(out=result[:], in_=acc[:])
+                        nc.sync.dma_start(out=out_view[:, h, cols], in_=result[:])

@@ -1,7 +1,6 @@
 from contextlib import ExitStack
 
 import concourse.mybir as mybir
-from concourse.masks import make_identity
 
 K, T, S, H, N, V = 1024, 2048, 1024, 512, 256, 512
 FLOPS = 2 * K * H * S + 2 * H * N * V
@@ -22,7 +21,7 @@ QUADRANT = 32
 SLICE = 256
 CHUNK = 128
 CHUNKS = V // CHUNK
-SCALAR_COLS = 320
+SCALAR_COLS = 256
 
 
 def tile_picked_phpool_none_p_kernel(tc, x_words, x_scales, w1, w2_words, w2_scales, offs, out):
@@ -36,7 +35,7 @@ def tile_picked_phpool_none_p_kernel(tc, x_words, x_scales, w1, w2_words, w2_sca
         offsets = keep.tile([P, S // 16], U16, name="offsets")
         nc.sync.dma_start(offsets[:], offs)
 
-        scale_table = keep.tile([P, T], U8, name="scale_table", tag="late_words", align_bytes=64)
+        scale_table = keep.tile([P, T], U8, name="scale_table", align_bytes=64)
         nc.vector.memset(scale_table[:].bitcast(I32), 0)
         nc.sync.dma_start(
             out=scale_table[0:P:4, :].bitcast(I32),
@@ -46,10 +45,20 @@ def tile_picked_phpool_none_p_kernel(tc, x_words, x_scales, w1, w2_words, w2_sca
         x_planes = keep.tile([P, PASSES, S], U8, name="x_planes", align_bytes=64)
         nc.vector.memset(x_planes[:].rearrange("p z s -> p (z s)").bitcast(I32), 0)
 
-        draft = reuse.tile([P, 1312], F32, name="draft", align_bytes=64, offset=8192 - 64)
-        make_identity(nc, draft[:, 0:P])
         identity = keep.tile([P, P], F32, name="identity", align_bytes=64)
-        nc.scalar.copy(identity[:], draft[:, 0:P])
+        for half, (offset, words) in enumerate(((17408, 64), (8192 - 64, 288))):
+            draft = reuse.tile([P, words], F32, name="draft%d" % half, align_bytes=64, offset=offset)
+            nc.gpsimd.memset(draft[:, 0:64], 0.0)
+            nc.gpsimd.affine_select(
+                out=draft[:, 0:64],
+                in_=draft[:, 0:64],
+                compare_op=mybir.AluOpType.not_equal,
+                fill=1.0,
+                base=-64 * half,
+                pattern=[[-1, 64]],
+                channel_multiplier=1,
+            )
+            nc.vector.tensor_copy(identity[:, 64 * half : 64 * half + 64], draft[:, 0:64])
 
         def load_words(z, table):
             nc.sync.dma_start(
@@ -63,13 +72,15 @@ def tile_picked_phpool_none_p_kernel(tc, x_words, x_scales, w1, w2_words, w2_sca
                 in_=w1[z * K_PASS : (z + 1) * K_PASS, :].rearrange("(p j) c -> p j c", j=PACK),
             )
 
-        raw0 = keep.tile([P, PACK, H], F32, name="raw0", tag="late_w2", align_bytes=64)
-        load_w1(0, raw0)
+        rows0 = w1[0:K_PASS, :].rearrange("(p j) c -> p j c", j=PACK)
+        raw0_low = keep.tile([P, 2, H], F32, name="raw0_low", align_bytes=64)
+        nc.sync.dma_start(out=raw0_low[:], in_=rows0[:, 0:2, :])
+        raw0_high = reuse.tile([P, 2, H], F32, name="raw0_high", align_bytes=64, offset=17408)
+        nc.sync.dma_start(out=raw0_high[:], in_=rows0[:, 2:4, :])
         table0 = reuse.tile([P, T], U32, name="table0", align_bytes=64, offset=0)
         load_words(0, table0)
-        raw1 = reuse.tile([P, PACK, H], F32, name="raw1", align_bytes=64, offset=13312)
+        raw1 = reuse.tile([P, PACK, H], F32, name="raw1", align_bytes=64, offset=9216)
         load_w1(1, raw1)
-        w1_raw = [raw0, raw1]
 
         picked_scales = reuse.tile([P, S], U8, name="picked_scales", align_bytes=64, offset=8192)
         nc.vector.tensor_copy(picked_scales[:], scale_table[:].indirect(offsets[:]))
@@ -79,9 +90,7 @@ def tile_picked_phpool_none_p_kernel(tc, x_words, x_scales, w1, w2_words, w2_sca
                 in_=picked_scales[QUADRANT * q : QUADRANT * (q + 1) : 4, :].bitcast(I32),
             )
 
-        table1 = keep.tile([P, T], U32, name="table1", tag="late_words", align_bytes=64)
-        load_words(1, table1)
-        word_table = [table0, table1]
+        word_table = [table0]
 
         w2_plane = reuse.tile([P, N], U8, name="w2_plane", align_bytes=64, offset=8192)
         nc.gpsimd.memset(w2_plane[:].bitcast(I32), 0)
@@ -95,17 +104,23 @@ def tile_picked_phpool_none_p_kernel(tc, x_words, x_scales, w1, w2_words, w2_sca
         w1_plane = [keep.tile([P, H], U8, name="w1_plane%d" % z, align_bytes=64) for z in range(PASSES)]
 
         def quantize_w1(z):
-            grouped = reuse.tile([P, H, PACK], BF16, name="w1_grouped%d" % z, align_bytes=64, offset=(9216, 21504)[z])
-            a, b = slice(0, SCALAR_COLS), slice(SCALAR_COLS, H)
-            nc.scalar.copy(
-                out=grouped[:, a, :].rearrange("p (c i) j -> p c j i", i=4),
-                in_=w1_raw[z][:, :, a].rearrange("p j (c i) -> p c j i", i=4),
-            )
-            second_copy = nc.scalar.copy if z == 0 else nc.vector.tensor_copy
-            second_copy(
-                out=grouped[:, b, :].rearrange("p (c i) j -> p c j i", i=4),
-                in_=w1_raw[z][:, :, b].rearrange("p j (c i) -> p c j i", i=4),
-            )
+            grouped = reuse.tile([P, H, PACK], BF16, name="w1_grouped%d" % z, align_bytes=64, offset=(25600, 29696)[z])
+            if z == 0:
+                for j0, raw in ((0, raw0_low), (2, raw0_high)):
+                    nc.scalar.copy(
+                        out=grouped[:, :, j0 : j0 + 2].rearrange("p (c i) j -> p c j i", i=2),
+                        in_=raw[:].rearrange("p j (c i) -> p c j i", i=2),
+                    )
+            else:
+                a, b = slice(0, SCALAR_COLS), slice(SCALAR_COLS, H)
+                nc.scalar.copy(
+                    out=grouped[:, a, :].rearrange("p (c i) j -> p c j i", i=2),
+                    in_=raw1[:, :, a].rearrange("p j (c i) -> p c j i", i=2),
+                )
+                nc.vector.tensor_copy(
+                    out=grouped[:, b, :].rearrange("p (c i) j -> p c j i", i=2),
+                    in_=raw1[:, :, b].rearrange("p j (c i) -> p c j i", i=2),
+                )
             nc.vector.quantize_mx(
                 out=w1_codes[z][:].bitcast(FP8X4),
                 scales=w1_plane[z][:],
@@ -132,19 +147,32 @@ def tile_picked_phpool_none_p_kernel(tc, x_words, x_scales, w1, w2_words, w2_sca
                     stop=(z == PASSES - 1),
                 )
 
-        first = [gather(0, s0, 25600 + 1024 * i) for i, s0 in enumerate(starts[:2])]
+        first = [gather(0, s0, 33792 + 1024 * i) for i, s0 in enumerate(starts[:2])]
         quantize_w1(0)
-        first = first + [gather(0, s0, 9216 + 1024 * i) for i, s0 in enumerate(starts[2:])]
-        w2_codes = keep.tile([P, N], U32, name="w2_codes", tag="late_w2", align_bytes=64)
+        table1 = reuse.tile([P, T], U32, name="table1", align_bytes=64, offset=17408)
+        load_words(1, table1)
+        word_table.append(table1)
+        for b in range(3):
+            nc.tensor.matmul_mx(
+                out=banks[CHUNKS - 1][:],
+                lhsT=w1_codes[0][:, 0:P].bitcast(FP8X4),
+                lhsT_scale=w1_plane[0][:, 0:P],
+                rhs=w1_codes[0][:].bitcast(FP8X4),
+                rhs_scale=w1_plane[0][:],
+                start=True,
+                stop=True,
+            )
+        first = first + [gather(0, s0, 25600 + 1024 * i) for i, s0 in enumerate(starts[2:])]
+        for s0, picked in zip(starts, first):
+            project(0, s0, picked)
+        quantize_w1(1)
+        w2_codes = reuse.tile([P, N], U32, name="w2_codes", align_bytes=64, offset=9216)
         nc.sync.dma_start(
             out=w2_codes[:].bitcast(I32),
             in_=w2_words[0].rearrange("p n t -> p (n t)").bitcast(I32),
         )
-        for s0, picked in zip(starts, first):
-            project(0, s0, picked)
-        quantize_w1(1)
         for i, s0 in enumerate(starts):
-            project(1, s0, gather(1, s0, 21504 + 1024 * i))
+            project(1, s0, gather(1, s0, 29696 + 1024 * i))
 
         order = "v (p u e) -> v u p e"
         split = "v (u p e) -> v u p e"
@@ -201,22 +229,22 @@ def tile_picked_phpool_none_p_kernel(tc, x_words, x_scales, w1, w2_words, w2_sca
             )
             z_plane = keep.tile([P, width], U8, name="z_plane%d" % g, align_bytes=64)
             nc.vector.quantize_mx(out=z_codes[:].bitcast(FP8X4), scales=z_plane[:], in_=z_grouped[g][:])
-            if g < len(groups) - 1:
-                acc = psum.tile([P, N // P, width], F32, name="acc%d" % g, tag="bank%d" % g)
+            if g == 1:
+                acc = psum.tile([P, N // P, width], F32, name="acc%d" % g, tag="bank2")
                 for h in range(N // P):
                     second_layer(acc[:, h, :], h, z_codes, z_plane)
                 result = keep.tile([P, N // P, width], F32, name="result%d" % g, align_bytes=64)
-                if g == 0:
-                    nc.scalar.copy(out=result[:], in_=acc[:])
-                else:
-                    nc.vector.tensor_copy(out=result[:], in_=acc[:])
+                nc.vector.tensor_copy(out=result[:], in_=acc[:])
                 nc.sync.dma_start(out=out_view[:, :, cols], in_=result[:])
             else:
                 for h in range(N // P):
-                    acc = psum.tile([P, width], F32, name="acc_last%d" % h, tag="bank%d" % (g + h))
+                    acc = psum.tile([P, width], F32, name="acc%d_%d" % (g, h), tag="bank%d" % (c0 + h))
                     second_layer(acc[:], h, z_codes, z_plane)
-                    result = keep.tile([P, width], F32, name="result_last%d" % h, align_bytes=64)
-                    if h == 0:
+                    result = keep.tile([P, width], F32, name="result%d_%d" % (g, h), align_bytes=64)
+                    if g == 0:
+                        nc.scalar.copy(out=result[:], in_=acc[:])
+                        nc.sync.dma_start(out=out_view[:, h, cols], in_=result[:])
+                    elif h == 0:
                         nc.scalar.copy(out=result[:], in_=acc[:])
                         nc.scalar.dma_start(out=out_view[:, h, cols], in_=result[:])
                     else:

@@ -21,7 +21,7 @@ QUADRANT = 32
 SLICE = 256
 CHUNK = 128
 CHUNKS = V // CHUNK
-SCALAR_COLS = 256
+SCALAR_M = 80
 
 
 def tile_picked_phpool_none_p_kernel(tc, x_words, x_scales, w1, w2_words, w2_scales, offs, out):
@@ -29,36 +29,37 @@ def tile_picked_phpool_none_p_kernel(tc, x_words, x_scales, w1, w2_words, w2_sca
     with ExitStack() as ctx:
         keep = ctx.enter_context(tc.tile_pool(name="keep", bufs=1))
         reuse = ctx.enter_context(tc.tile_pool(name="reuse", bufs=1))
-        tail = ctx.enter_context(tc.tile_pool(name="tail", bufs=1))
+        early = ctx.enter_context(tc.tile_pool(name="early", bufs=1))
+        stage = ctx.enter_context(tc.tile_pool(name="stage", bufs=1))
         psum = ctx.enter_context(tc.psum_pool(name="psum", bufs=1))
 
         offsets = keep.tile([P, S // 16], U16, name="offsets")
         nc.sync.dma_start(offsets[:], offs)
 
-        scale_table = keep.tile([P, T], U8, name="scale_table", align_bytes=64)
+        scale_table = reuse.tile([P, T], U8, name="scale_table", align_bytes=64, offset=7168)
         nc.vector.memset(scale_table[:].bitcast(I32), 0)
         nc.sync.dma_start(
             out=scale_table[0:P:4, :].bitcast(I32),
             in_=x_scales.rearrange("z q c -> q z c").bitcast(I32),
         )
 
+        w2_plane = keep.tile([P, N], U8, name="w2_plane", align_bytes=64)
+
+        def clear_w2_plane(half, pool, offset):
+            zeros = pool.tile([P, N // 2], U8, name="zeros%d" % half, align_bytes=64, offset=offset)
+            nc.vector.memset(zeros[:].bitcast(I32), 0)
+            nc.vector.tensor_copy(w2_plane[:, half * N // 2 : (half + 1) * N // 2].bitcast(I32), zeros[:].bitcast(I32))
+
+        clear_w2_plane(0, early, 12288 - N // 4)
+        clear_w2_plane(1, early, 20480)
+        for q in range(4):
+            nc.gpsimd.dma_start(
+                out=w2_plane[QUADRANT * q : QUADRANT * q + 4, :].bitcast(I32),
+                in_=w2_scales[0, 4 * q : 4 * q + 4, :].bitcast(I32),
+            )
+
         x_planes = keep.tile([P, PASSES, S], U8, name="x_planes", align_bytes=64)
         nc.vector.memset(x_planes[:].rearrange("p z s -> p (z s)").bitcast(I32), 0)
-
-        identity = keep.tile([P, P], F32, name="identity", align_bytes=64)
-        for half, (offset, words) in enumerate(((17408, 64), (8192 - 64, 288))):
-            draft = reuse.tile([P, words], F32, name="draft%d" % half, align_bytes=64, offset=offset)
-            nc.gpsimd.memset(draft[:, 0:64], 0.0)
-            nc.gpsimd.affine_select(
-                out=draft[:, 0:64],
-                in_=draft[:, 0:64],
-                compare_op=mybir.AluOpType.not_equal,
-                fill=1.0,
-                base=-64 * half,
-                pattern=[[-1, 64]],
-                channel_multiplier=1,
-            )
-            nc.vector.tensor_copy(identity[:, 64 * half : 64 * half + 64], draft[:, 0:64])
 
         def load_words(z, table):
             nc.sync.dma_start(
@@ -66,23 +67,19 @@ def tile_picked_phpool_none_p_kernel(tc, x_words, x_scales, w1, w2_words, w2_sca
                 in_=x_words[z].rearrange("p n t -> p (n t)").bitcast(I32),
             )
 
-        def load_w1(z, raw):
-            nc.sync.dma_start(
-                out=raw[:],
-                in_=w1[z * K_PASS : (z + 1) * K_PASS, :].rearrange("(p j) c -> p j c", j=PACK),
-            )
+        def load_w1(z, m0, m1, pool, offset):
+            raw = pool.tile([P, PACK, PACK * (m1 - m0)], F32, name="raw%d_%d" % (z, m0), align_bytes=64, offset=offset)
+            rows = w1[z * K_PASS : (z + 1) * K_PASS, PACK * m0 : PACK * m1]
+            nc.sync.dma_start(out=raw[:], in_=rows.rearrange("(p j) c -> p j c", j=PACK))
+            return raw
 
-        rows0 = w1[0:K_PASS, :].rearrange("(p j) c -> p j c", j=PACK)
-        raw0_low = keep.tile([P, 2, H], F32, name="raw0_low", align_bytes=64)
-        nc.sync.dma_start(out=raw0_low[:], in_=rows0[:, 0:2, :])
-        raw0_high = reuse.tile([P, 2, H], F32, name="raw0_high", align_bytes=64, offset=17408)
-        nc.sync.dma_start(out=raw0_high[:], in_=rows0[:, 2:4, :])
-        table0 = reuse.tile([P, T], U32, name="table0", align_bytes=64, offset=0)
+        raw0_scalar = load_w1(0, 0, P // 2, reuse, 0)
+        raw0_vector = load_w1(0, P // 2, P, early, 8192)
+        table0 = early.tile([P, T], U32, name="table0", align_bytes=64, offset=12288)
         load_words(0, table0)
-        raw1 = reuse.tile([P, PACK, H], F32, name="raw1", align_bytes=64, offset=9216)
-        load_w1(1, raw1)
+        raw1_scalar = load_w1(1, 0, SCALAR_M, early, 20480)
 
-        picked_scales = reuse.tile([P, S], U8, name="picked_scales", align_bytes=64, offset=8192)
+        picked_scales = reuse.tile([P, S], U8, name="picked_scales", align_bytes=64, offset=17408)
         nc.vector.tensor_copy(picked_scales[:], scale_table[:].indirect(offsets[:]))
         for q in range(4):
             nc.sync.dma_start(
@@ -92,161 +89,107 @@ def tile_picked_phpool_none_p_kernel(tc, x_words, x_scales, w1, w2_words, w2_sca
 
         word_table = [table0]
 
-        w2_plane = reuse.tile([P, N], U8, name="w2_plane", align_bytes=64, offset=8192)
-        nc.gpsimd.memset(w2_plane[:].bitcast(I32), 0)
-        for q in range(4):
-            nc.sync.dma_start(
-                out=w2_plane[QUADRANT * q : QUADRANT * q + 4, :].bitcast(I32),
-                in_=w2_scales[0, 4 * q : 4 * q + 4, :].bitcast(I32),
-            )
+        w2_codes = reuse.tile([P, N], U32, name="w2_codes", align_bytes=64, offset=17408 + N)
+        nc.sync.dma_start(
+            out=w2_codes[:].bitcast(I32),
+            in_=w2_words[0].rearrange("p n t -> p (n t)").bitcast(I32),
+        )
 
         w1_codes = [keep.tile([P, H], U32, name="w1_codes%d" % z, align_bytes=64) for z in range(PASSES)]
         w1_plane = [keep.tile([P, H], U8, name="w1_plane%d" % z, align_bytes=64) for z in range(PASSES)]
 
-        def quantize_w1(z):
-            grouped = reuse.tile([P, H, PACK], BF16, name="w1_grouped%d" % z, align_bytes=64, offset=(25600, 29696)[z])
-            if z == 0:
-                for j0, raw in ((0, raw0_low), (2, raw0_high)):
-                    nc.scalar.copy(
-                        out=grouped[:, :, j0 : j0 + 2].rearrange("p (c i) j -> p c j i", i=2),
-                        in_=raw[:].rearrange("p j (c i) -> p c j i", i=2),
-                    )
-            else:
-                a, b = slice(0, SCALAR_COLS), slice(SCALAR_COLS, H)
-                nc.scalar.copy(
-                    out=grouped[:, a, :].rearrange("p (c i) j -> p c j i", i=2),
-                    in_=raw1[:, :, a].rearrange("p j (c i) -> p c j i", i=2),
-                )
-                nc.vector.tensor_copy(
-                    out=grouped[:, b, :].rearrange("p (c i) j -> p c j i", i=2),
-                    in_=raw1[:, :, b].rearrange("p j (c i) -> p c j i", i=2),
+        def quantize_w1(z, split, low, high):
+            grouped = stage.tile([P, PACK, P, PACK], BF16, name="w1_grouped%d" % z, align_bytes=64, offset=4096 * z)
+            for copy, m0, m1, raw in ((nc.scalar.copy, 0, split, low), (nc.vector.tensor_copy, split, P, high)):
+                copy(
+                    out=grouped[:, :, m0:m1, :].rearrange("p t m j -> p m t j"),
+                    in_=raw[:].rearrange("p j (m t) -> p m t j", t=PACK),
                 )
             nc.vector.quantize_mx(
                 out=w1_codes[z][:].bitcast(FP8X4),
                 scales=w1_plane[z][:],
-                in_=grouped[:].rearrange("p c j -> p (c j)"),
+                in_=grouped[:].rearrange("p t m j -> p (t m j)"),
             )
 
-        banks = [psum.tile([P, H], F32, name="bank%d" % b, tag="bank%d" % b) for b in range(2 * CHUNKS)]
+        banks = [psum.tile([P, PACK, CHUNK], F32, name="bank%d" % b, tag="bank%d" % b) for b in range(2 * CHUNKS)]
         starts = [V, 0, V + SLICE, SLICE]
 
-        def gather(z, s0, offset):
-            picked = reuse.tile([P, SLICE], U32, name="picked%d_%d" % (z, s0), align_bytes=64, offset=offset)
+        def gather(z, s0):
+            picked = stage.tile(
+                [P, SLICE], U32, name="picked%d_%d" % (z, s0), align_bytes=64, offset=4096 * z + 4 * s0
+            )
             nc.vector.tensor_copy(picked[:], word_table[z][:].indirect(offsets[:, s0 // 16 : (s0 + SLICE) // 16]))
             return picked
 
         def project(z, s0, picked):
             for c0 in range(0, SLICE, CHUNK):
-                nc.tensor.matmul_mx(
-                    out=banks[(s0 + c0) // CHUNK][:],
-                    lhsT=picked[:, c0 : c0 + CHUNK].bitcast(FP8X4),
-                    lhsT_scale=x_planes[:, z, s0 + c0 : s0 + c0 + CHUNK],
-                    rhs=w1_codes[z][:].bitcast(FP8X4),
-                    rhs_scale=w1_plane[z][:],
-                    start=(z == 0),
-                    stop=(z == PASSES - 1),
-                )
+                for t in range(PACK):
+                    nc.tensor.matmul_mx(
+                        out=banks[(s0 + c0) // CHUNK][:, t, :],
+                        lhsT=w1_codes[z][:, t * P : (t + 1) * P].bitcast(FP8X4),
+                        lhsT_scale=w1_plane[z][:, t * P : (t + 1) * P],
+                        rhs=picked[:, c0 : c0 + CHUNK].bitcast(FP8X4),
+                        rhs_scale=x_planes[:, z, s0 + c0 : s0 + c0 + CHUNK],
+                        start=(z == 0 and t == 0),
+                        stop=(z == PASSES - 1 and t == PACK - 1),
+                    )
 
-        first = [gather(0, s0, 33792 + 1024 * i) for i, s0 in enumerate(starts[:2])]
-        quantize_w1(0)
-        table1 = reuse.tile([P, T], U32, name="table1", align_bytes=64, offset=17408)
+        quantize_w1(0, P // 2, raw0_scalar, raw0_vector)
+        raw1_vector = load_w1(1, SCALAR_M, P, early, 9216)
+        table1 = early.tile([P, T], U32, name="table1", align_bytes=64, offset=1024)
         load_words(1, table1)
         word_table.append(table1)
-        for b in range(3):
-            nc.tensor.matmul_mx(
-                out=banks[CHUNKS - 1][:],
-                lhsT=w1_codes[0][:, 0:P].bitcast(FP8X4),
-                lhsT_scale=w1_plane[0][:, 0:P],
-                rhs=w1_codes[0][:].bitcast(FP8X4),
-                rhs_scale=w1_plane[0][:],
-                start=True,
-                stop=True,
-            )
-        first = first + [gather(0, s0, 25600 + 1024 * i) for i, s0 in enumerate(starts[2:])]
-        for s0, picked in zip(starts, first):
-            project(0, s0, picked)
-        quantize_w1(1)
-        w2_codes = reuse.tile([P, N], U32, name="w2_codes", align_bytes=64, offset=9216)
-        nc.sync.dma_start(
-            out=w2_codes[:].bitcast(I32),
-            in_=w2_words[0].rearrange("p n t -> p (n t)").bitcast(I32),
-        )
-        for i, s0 in enumerate(starts):
-            project(1, s0, gather(1, s0, 29696 + 1024 * i))
+        for s0 in starts:
+            project(0, s0, gather(0, s0))
+        quantize_w1(1, SCALAR_M, raw1_scalar, raw1_vector)
+        for s0 in starts:
+            project(1, s0, gather(1, s0))
 
-        order = "v (p u e) -> v u p e"
-        split = "v (u p e) -> v u p e"
         seconds = []
         for c in range(CHUNKS):
-            second = tail.tile([P, H], F32, name="second%d" % c, align_bytes=64, offset=2048 * c)
-            nc.scalar.copy(
-                out=second[:].rearrange(split, u=2, e=2),
-                in_=banks[CHUNKS + c][:].rearrange(order, u=2, e=2),
-            )
+            second = keep.tile([P, CHUNK, PACK], F32, name="second%d" % c, align_bytes=64)
+            nc.scalar.copy(out=second[:], in_=banks[CHUNKS + c][:].rearrange("p t v -> p v t"))
             seconds.append(second)
 
-        groups = [(0, 2), (2, 3), (3, 4)]
-        z_grouped = [
-            keep.tile([P, (c1 - c0) * CHUNK * PACK], BF16, name="z_grouped%d" % c0, align_bytes=64)
-            for c0, c1 in groups
-        ]
-        for g, (c0, c1) in enumerate(groups):
-            for c in range(c0, c1):
-                z_rows = keep.tile([P, H], BF16, name="z_rows%d" % c, align_bytes=64)
-                nc.vector.tensor_tensor(
-                    out=z_rows[:].rearrange(split, u=2, e=2),
-                    in0=banks[c][:].rearrange(order, u=2, e=2),
-                    in1=seconds[c][:].rearrange(split, u=2, e=2),
-                    op=mybir.AluOpType.max,
-                )
-                pairs = z_rows[:].bitcast(F32)
-                turned = psum.tile([P, 2, CHUNK], F32, name="turned%d" % c, tag="bank%d" % (CHUNKS + c))
-                for u in range(2):
-                    nc.tensor.transpose(turned[:, u, :], pairs[:, u * P : (u + 1) * P], identity[:])
-                words = z_grouped[g][:].bitcast(F32)[:, (c - c0) * 2 * CHUNK : (c - c0 + 1) * 2 * CHUNK]
-                nc.scalar.copy(
-                    out=words.rearrange("p (v u) -> p v u", u=2),
-                    in_=turned[:].rearrange("p u v -> p v u"),
-                )
-
-        def second_layer(acc, h, z_codes, z_plane):
-            nc.tensor.matmul_mx(
-                out=acc,
-                lhsT=w2_codes[:, h * P : (h + 1) * P].bitcast(FP8X4),
-                lhsT_scale=w2_plane[:, h * P : (h + 1) * P],
-                rhs=z_codes[:].bitcast(FP8X4),
-                rhs_scale=z_plane[:],
-                start=True,
-                stop=True,
-            )
-
         out_view = out.rearrange("(h p) v -> p h v", p=P)
+        groups = [(0, 2), (2, 3), (3, 4)]
         for g, (c0, c1) in enumerate(groups):
             width = (c1 - c0) * CHUNK
             cols = slice(c0 * CHUNK, c1 * CHUNK)
-            z_codes = tail.tile(
-                [P, width], U32, name="z_codes%d" % g, align_bytes=64, offset=2048 * (CHUNKS - 1) + 4 * c0 * CHUNK
-            )
+            z_grouped = keep.tile([P, width, PACK], BF16, name="z_grouped%d" % g, align_bytes=64)
+            for c in range(c0, c1):
+                nc.vector.tensor_tensor(
+                    out=z_grouped[:, (c - c0) * CHUNK : (c - c0 + 1) * CHUNK, :],
+                    in0=banks[c][:].rearrange("p t v -> p v t"),
+                    in1=seconds[c][:],
+                    op=mybir.AluOpType.max,
+                )
+            z_codes = keep.tile([P, width], U32, name="z_codes%d" % g, align_bytes=64)
             z_plane = keep.tile([P, width], U8, name="z_plane%d" % g, align_bytes=64)
-            nc.vector.quantize_mx(out=z_codes[:].bitcast(FP8X4), scales=z_plane[:], in_=z_grouped[g][:])
-            if g == 1:
-                acc = psum.tile([P, N // P, width], F32, name="acc%d" % g, tag="bank2")
-                for h in range(N // P):
-                    second_layer(acc[:, h, :], h, z_codes, z_plane)
-                result = keep.tile([P, N // P, width], F32, name="result%d" % g, align_bytes=64)
-                nc.vector.tensor_copy(out=result[:], in_=acc[:])
-                nc.sync.dma_start(out=out_view[:, :, cols], in_=result[:])
+            nc.vector.quantize_mx(
+                out=z_codes[:].bitcast(FP8X4), scales=z_plane[:], in_=z_grouped[:].rearrange("p v t -> p (v t)")
+            )
+            last = g == len(groups) - 1
+            accs = [
+                psum.tile([P, N // P, width], F32, name="acc%d_%d" % (g, b), tag="bank%d" % (CHUNKS + c0 - CHUNKS * b))
+                for b in range(2 if last else 1)
+            ]
+            for h in range(N // P):
+                nc.tensor.matmul_mx(
+                    out=accs[h if last else 0][:, h, :],
+                    lhsT=w2_codes[:, h * P : (h + 1) * P].bitcast(FP8X4),
+                    lhsT_scale=w2_plane[:, h * P : (h + 1) * P],
+                    rhs=z_codes[:].bitcast(FP8X4),
+                    rhs_scale=z_plane[:],
+                    start=True,
+                    stop=True,
+                )
+            if last:
+                for h, copy, queue in ((0, nc.scalar.copy, nc.scalar), (1, nc.vector.tensor_copy, nc.sync)):
+                    half = keep.tile([P, width], F32, name="half%d" % h, align_bytes=64)
+                    copy(out=half[:], in_=accs[h][:, h, :])
+                    queue.dma_start(out=out_view[:, h, cols], in_=half[:])
             else:
-                for h in range(N // P):
-                    acc = psum.tile([P, width], F32, name="acc%d_%d" % (g, h), tag="bank%d" % (c0 + h))
-                    second_layer(acc[:], h, z_codes, z_plane)
-                    result = keep.tile([P, width], F32, name="result%d_%d" % (g, h), align_bytes=64)
-                    if g == 0:
-                        nc.scalar.copy(out=result[:], in_=acc[:])
-                        nc.sync.dma_start(out=out_view[:, h, cols], in_=result[:])
-                    elif h == 0:
-                        nc.scalar.copy(out=result[:], in_=acc[:])
-                        nc.scalar.dma_start(out=out_view[:, h, cols], in_=result[:])
-                    else:
-                        nc.vector.tensor_copy(out=result[:], in_=acc[:])
-                        nc.sync.dma_start(out=out_view[:, h, cols], in_=result[:])
+                result = keep.tile([P, N // P, width], F32, name="result%d" % g, align_bytes=64)
+                nc.scalar.copy(out=result[:], in_=accs[0][:])
+                nc.sync.dma_start(out=out_view[:, :, cols], in_=result[:])

@@ -33,34 +33,6 @@ def tile_picked_phpool_none_p_kernel(tc, x_words, x_scales, w1, w2_words, w2_sca
         stage = ctx.enter_context(tc.tile_pool(name="stage", bufs=1))
         psum = ctx.enter_context(tc.psum_pool(name="psum", bufs=1))
 
-        offsets = keep.tile([P, S // 16], U16, name="offsets")
-        nc.sync.dma_start(offsets[:], offs)
-
-        scale_table = reuse.tile([P, T], U8, name="scale_table", align_bytes=64, offset=7168)
-        nc.vector.memset(scale_table[:].bitcast(I32), 0)
-        nc.sync.dma_start(
-            out=scale_table[0:P:4, :].bitcast(I32),
-            in_=x_scales.rearrange("z q c -> q z c").bitcast(I32),
-        )
-
-        w2_plane = keep.tile([P, N], U8, name="w2_plane", align_bytes=64)
-
-        def clear_w2_plane(half, pool, offset):
-            zeros = pool.tile([P, N // 2], U8, name="zeros%d" % half, align_bytes=64, offset=offset)
-            nc.vector.memset(zeros[:].bitcast(I32), 0)
-            nc.vector.tensor_copy(w2_plane[:, half * N // 2 : (half + 1) * N // 2].bitcast(I32), zeros[:].bitcast(I32))
-
-        clear_w2_plane(0, early, 12288 - N // 4)
-        clear_w2_plane(1, early, 20480)
-        for q in range(4):
-            nc.gpsimd.dma_start(
-                out=w2_plane[QUADRANT * q : QUADRANT * q + 4, :].bitcast(I32),
-                in_=w2_scales[0, 4 * q : 4 * q + 4, :].bitcast(I32),
-            )
-
-        x_planes = keep.tile([P, PASSES, S], U8, name="x_planes", align_bytes=64)
-        nc.vector.memset(x_planes[:].rearrange("p z s -> p (z s)").bitcast(I32), 0)
-
         def load_words(z, table):
             nc.sync.dma_start(
                 out=table[:].bitcast(I32),
@@ -73,13 +45,30 @@ def tile_picked_phpool_none_p_kernel(tc, x_words, x_scales, w1, w2_words, w2_sca
             nc.sync.dma_start(out=raw[:], in_=rows.rearrange("(p j) c -> p j c", j=PACK))
             return raw
 
-        raw0_scalar = load_w1(0, 0, P // 2, reuse, 0)
-        raw0_vector = load_w1(0, P // 2, P, early, 8192)
-        table0 = early.tile([P, T], U32, name="table0", align_bytes=64, offset=12288)
-        load_words(0, table0)
-        raw1_scalar = load_w1(1, 0, SCALAR_M, early, 20480)
+        raw0_scalar = load_w1(0, 0, P // 2, early, 25600)
 
-        picked_scales = reuse.tile([P, S], U8, name="picked_scales", align_bytes=64, offset=17408)
+        offsets = keep.tile([P, S // 16], U16, name="offsets")
+        nc.sync.dma_start(offsets[:], offs)
+
+        scale_table = keep.tile([P, T], U8, name="scale_table", align_bytes=64)
+        nc.vector.memset(scale_table[:].bitcast(I32), 0)
+        nc.sync.dma_start(
+            out=scale_table[0:P:4, :].bitcast(I32),
+            in_=x_scales.rearrange("z q c -> q z c").bitcast(I32),
+        )
+
+        x_planes = keep.tile([P, PASSES, S], U8, name="x_planes", align_bytes=64)
+        for z, offset in enumerate((4096 - S // 2, 12288)):
+            zeros = early.tile([P, S], U8, name="zeros%d" % z, align_bytes=64, offset=offset)
+            nc.vector.memset(zeros[:].bitcast(I32), 0)
+            nc.vector.tensor_copy(x_planes[:, z, :].bitcast(I32), zeros[:].bitcast(I32))
+
+        raw0_vector = load_w1(0, P // 2, P, early, 0)
+        table0 = early.tile([P, T], U32, name="table0", align_bytes=64, offset=4096)
+        load_words(0, table0)
+        raw1_scalar = load_w1(1, 0, SCALAR_M, early, 12288)
+
+        picked_scales = reuse.tile([P, S], U8, name="picked_scales", align_bytes=64, offset=0)
         nc.vector.tensor_copy(picked_scales[:], scale_table[:].indirect(offsets[:]))
         for q in range(4):
             nc.sync.dma_start(
@@ -88,12 +77,6 @@ def tile_picked_phpool_none_p_kernel(tc, x_words, x_scales, w1, w2_words, w2_sca
             )
 
         word_table = [table0]
-
-        w2_codes = reuse.tile([P, N], U32, name="w2_codes", align_bytes=64, offset=17408 + N)
-        nc.sync.dma_start(
-            out=w2_codes[:].bitcast(I32),
-            in_=w2_words[0].rearrange("p n t -> p (n t)").bitcast(I32),
-        )
 
         w1_codes = [keep.tile([P, H], U32, name="w1_codes%d" % z, align_bytes=64) for z in range(PASSES)]
         w1_plane = [keep.tile([P, H], U8, name="w1_plane%d" % z, align_bytes=64) for z in range(PASSES)]
@@ -121,8 +104,8 @@ def tile_picked_phpool_none_p_kernel(tc, x_words, x_scales, w1, w2_words, w2_sca
             nc.vector.tensor_copy(picked[:], word_table[z][:].indirect(offsets[:, s0 // 16 : (s0 + SLICE) // 16]))
             return picked
 
-        def project(z, s0, picked):
-            for c0 in range(0, SLICE, CHUNK):
+        def project(z, s0, picked, chunks=(0, CHUNK)):
+            for c0 in chunks:
                 for t in range(PACK):
                     nc.tensor.matmul_mx(
                         out=banks[(s0 + c0) // CHUNK][:, t, :],
@@ -135,33 +118,64 @@ def tile_picked_phpool_none_p_kernel(tc, x_words, x_scales, w1, w2_words, w2_sca
                     )
 
         quantize_w1(0, P // 2, raw0_scalar, raw0_vector)
-        raw1_vector = load_w1(1, SCALAR_M, P, early, 9216)
-        table1 = early.tile([P, T], U32, name="table1", align_bytes=64, offset=1024)
+        raw1_vector = load_w1(1, SCALAR_M, P, early, 26624)
+        table1 = early.tile([P, T], U32, name="table1", align_bytes=64, offset=18432)
         load_words(1, table1)
         word_table.append(table1)
-        for s0 in starts:
+
+        w2_plane = reuse.tile([P, N], U8, name="w2_plane", align_bytes=64, offset=0)
+        nc.vector.memset(w2_plane[:].bitcast(I32), 0)
+        for q in range(4):
+            nc.sync.dma_start(
+                out=w2_plane[QUADRANT * q : QUADRANT * q + 4, :].bitcast(I32),
+                in_=w2_scales[0, 4 * q : 4 * q + 4, :].bitcast(I32),
+            )
+        w2_codes = reuse.tile([P, N], U32, name="w2_codes", align_bytes=64, offset=N)
+        nc.sync.dma_start(
+            out=w2_codes[:].bitcast(I32),
+            in_=w2_words[0].rearrange("p n t -> p (n t)").bitcast(I32),
+        )
+
+        for s0 in starts[:-1]:
             project(0, s0, gather(0, s0))
+        last_picked = gather(0, starts[-1])
+        project(0, starts[-1], last_picked, (0,))
         quantize_w1(1, SCALAR_M, raw1_scalar, raw1_vector)
+        for warm in range(3):
+            nc.tensor.matmul_mx(
+                out=banks[CHUNKS - 1][:].rearrange("p t v -> p (t v)"),
+                lhsT=w1_codes[1][:, 0:P].bitcast(FP8X4),
+                lhsT_scale=w1_plane[1][:, 0:P],
+                rhs=w1_codes[1][:].bitcast(FP8X4),
+                rhs_scale=w1_plane[1][:],
+                start=True,
+                stop=True,
+            )
+        project(0, starts[-1], last_picked, (CHUNK,))
         for s0 in starts:
             project(1, s0, gather(1, s0))
 
-        seconds = []
-        for c in range(CHUNKS):
-            second = keep.tile([P, CHUNK, PACK], F32, name="second%d" % c, align_bytes=64)
-            nc.scalar.copy(out=second[:], in_=banks[CHUNKS + c][:].rearrange("p t v -> p v t"))
-            seconds.append(second)
+        def rounded(b):
+            values = keep.tile([P, CHUNK, PACK], BF16, name="rounded%d" % b, align_bytes=64)
+            nc.scalar.copy(out=values[:], in_=banks[b][:].rearrange("p t v -> p v t"))
+            return values[:]
+
+        seconds = [rounded(CHUNKS + c) for c in range(CHUNKS)]
+        firsts = [banks[c][:].rearrange("p t v -> p v t") for c in range(CHUNKS - 1)] + [rounded(CHUNKS - 1)]
 
         out_view = out.rearrange("(h p) v -> p h v", p=P)
         groups = [(0, 2), (2, 3), (3, 4)]
         for g, (c0, c1) in enumerate(groups):
             width = (c1 - c0) * CHUNK
             cols = slice(c0 * CHUNK, c1 * CHUNK)
-            z_grouped = keep.tile([P, width, PACK], BF16, name="z_grouped%d" % g, align_bytes=64)
+            z_grouped = reuse.tile(
+                [P, width, PACK], BF16, name="z_grouped%d" % g, align_bytes=64, offset=(2048, 4096, 2048)[g]
+            )
             for c in range(c0, c1):
                 nc.vector.tensor_tensor(
                     out=z_grouped[:, (c - c0) * CHUNK : (c - c0 + 1) * CHUNK, :],
-                    in0=banks[c][:].rearrange("p t v -> p v t"),
-                    in1=seconds[c][:],
+                    in0=firsts[c],
+                    in1=seconds[c],
                     op=mybir.AluOpType.max,
                 )
             z_codes = keep.tile([P, width], U32, name="z_codes%d" % g, align_bytes=64)
@@ -184,12 +198,10 @@ def tile_picked_phpool_none_p_kernel(tc, x_words, x_scales, w1, w2_words, w2_sca
                     start=True,
                     stop=True,
                 )
+            result = keep.tile([P, N // P, width], F32, name="result%d" % g, align_bytes=64)
             if last:
-                for h, copy, queue in ((0, nc.scalar.copy, nc.scalar), (1, nc.vector.tensor_copy, nc.sync)):
-                    half = keep.tile([P, width], F32, name="half%d" % h, align_bytes=64)
-                    copy(out=half[:], in_=accs[h][:, h, :])
-                    queue.dma_start(out=out_view[:, h, cols], in_=half[:])
+                nc.scalar.copy(out=result[:, 0, :], in_=accs[0][:, 0, :])
+                nc.vector.tensor_copy(out=result[:, 1, :], in_=accs[1][:, 1, :])
             else:
-                result = keep.tile([P, N // P, width], F32, name="result%d" % g, align_bytes=64)
                 nc.scalar.copy(out=result[:], in_=accs[0][:])
-                nc.sync.dma_start(out=out_view[:, :, cols], in_=result[:])
+            nc.sync.dma_start(out=out_view[:, :, cols], in_=result[:])

@@ -22,6 +22,7 @@ SLICE = 256
 CHUNK = 128
 CHUNKS = V // CHUNK
 SCALAR_M = 80
+RUN = 4
 
 
 def tile_picked_phpool_none_p_kernel(tc, x_words, x_scales, w1, w2_words, w2_scales, offs, out):
@@ -104,8 +105,8 @@ def tile_picked_phpool_none_p_kernel(tc, x_words, x_scales, w1, w2_words, w2_sca
             nc.vector.tensor_copy(picked[:], word_table[z][:].indirect(offsets[:, s0 // 16 : (s0 + SLICE) // 16]))
             return picked
 
-        def project(z, s0, picked, chunks=(0, CHUNK)):
-            for c0 in chunks:
+        def project(z, s0, picked):
+            for c0 in range(0, SLICE, CHUNK):
                 for t in range(PACK):
                     nc.tensor.matmul_mx(
                         out=banks[(s0 + c0) // CHUNK][:, t, :],
@@ -124,7 +125,7 @@ def tile_picked_phpool_none_p_kernel(tc, x_words, x_scales, w1, w2_words, w2_sca
         word_table.append(table1)
 
         w2_plane = reuse.tile([P, N], U8, name="w2_plane", align_bytes=64, offset=0)
-        nc.vector.memset(w2_plane[:].bitcast(I32), 0)
+        nc.gpsimd.memset(w2_plane[:].bitcast(I32), 0)
         for q in range(4):
             nc.sync.dma_start(
                 out=w2_plane[QUADRANT * q : QUADRANT * q + 4, :].bitcast(I32),
@@ -136,32 +137,31 @@ def tile_picked_phpool_none_p_kernel(tc, x_words, x_scales, w1, w2_words, w2_sca
             in_=w2_words[0].rearrange("p n t -> p (n t)").bitcast(I32),
         )
 
-        for s0 in starts[:-1]:
+        for s0 in starts:
             project(0, s0, gather(0, s0))
-        last_picked = gather(0, starts[-1])
-        project(0, starts[-1], last_picked, (0,))
         quantize_w1(1, SCALAR_M, raw1_scalar, raw1_vector)
-        for warm in range(3):
-            nc.tensor.matmul_mx(
-                out=banks[CHUNKS - 1][:].rearrange("p t v -> p (t v)"),
-                lhsT=w1_codes[1][:, 0:P].bitcast(FP8X4),
-                lhsT_scale=w1_plane[1][:, 0:P],
-                rhs=w1_codes[1][:].bitcast(FP8X4),
-                rhs_scale=w1_plane[1][:],
-                start=True,
-                stop=True,
-            )
-        project(0, starts[-1], last_picked, (CHUNK,))
         for s0 in starts:
             project(1, s0, gather(1, s0))
 
-        def rounded(b):
-            values = keep.tile([P, CHUNK, PACK], BF16, name="rounded%d" % b, align_bytes=64)
-            nc.scalar.copy(out=values[:], in_=banks[b][:].rearrange("p t v -> p v t"))
+        def walk_bank(b):
+            return banks[b][:].rearrange("p t (w i) -> p w t i", i=RUN)
+
+        def walk_words(tile_ap):
+            return tile_ap.rearrange("p (w i) t -> p w t i", i=RUN)
+
+        def rounded_in_walk_order(b):
+            values = keep.tile([P, CHUNK // RUN, PACK, RUN], BF16, name="rounded%d" % b, align_bytes=64)
+            nc.scalar.copy(out=values[:], in_=walk_bank(b))
             return values[:]
 
-        seconds = [rounded(CHUNKS + c) for c in range(CHUNKS)]
-        firsts = [banks[c][:].rearrange("p t v -> p v t") for c in range(CHUNKS - 1)] + [rounded(CHUNKS - 1)]
+        def rounded_in_word_order(b):
+            values = keep.tile([P, CHUNK, PACK], BF16, name="rounded%d" % b, align_bytes=64)
+            nc.scalar.copy(out=walk_words(values[:]), in_=walk_bank(b))
+            return values[:]
+
+        seconds = [rounded_in_walk_order(CHUNKS + c) for c in range(CHUNKS - 1)]
+        seconds.append(rounded_in_word_order(2 * CHUNKS - 1))
+        firsts = [walk_bank(c) for c in range(CHUNKS - 1)] + [rounded_in_word_order(CHUNKS - 1)]
 
         out_view = out.rearrange("(h p) v -> p h v", p=P)
         groups = [(0, 2), (2, 3), (3, 4)]
@@ -169,11 +169,12 @@ def tile_picked_phpool_none_p_kernel(tc, x_words, x_scales, w1, w2_words, w2_sca
             width = (c1 - c0) * CHUNK
             cols = slice(c0 * CHUNK, c1 * CHUNK)
             z_grouped = reuse.tile(
-                [P, width, PACK], BF16, name="z_grouped%d" % g, align_bytes=64, offset=(2048, 4096, 2048)[g]
+                [P, width, PACK], BF16, name="z_grouped%d" % g, align_bytes=64, offset=(2048, 2048, 4096)[g]
             )
             for c in range(c0, c1):
+                z_chunk = z_grouped[:, (c - c0) * CHUNK : (c - c0 + 1) * CHUNK, :]
                 nc.vector.tensor_tensor(
-                    out=z_grouped[:, (c - c0) * CHUNK : (c - c0 + 1) * CHUNK, :],
+                    out=walk_words(z_chunk) if c < CHUNKS - 1 else z_chunk,
                     in0=firsts[c],
                     in1=seconds[c],
                     op=mybir.AluOpType.max,

@@ -22,6 +22,7 @@ SLICE = 256
 CHUNK = 128
 CHUNKS = V // CHUNK
 SCALAR_M = 80
+VECTOR_M = 96
 RUN = 4
 
 
@@ -53,41 +54,53 @@ def tile_picked_phpool_none_p_kernel(tc, x_words, x_scales, w1, w2_words, w2_sca
 
         scale_table = keep.tile([P, T], U8, name="scale_table", align_bytes=64)
         nc.vector.memset(scale_table[:].bitcast(I32), 0)
-        nc.sync.dma_start(
-            out=scale_table[0:P:4, :].bitcast(I32),
-            in_=x_scales.rearrange("z q c -> q z c").bitcast(I32),
-        )
+        for r in range(2):
+            nc.sync.dma_start(
+                out=scale_table[r:P:8, :].bitcast(I32),
+                in_=x_scales.rearrange("z (g r) c -> r g z c", r=2)[r].bitcast(I32),
+            )
 
-        x_planes = keep.tile([P, PASSES, S], U8, name="x_planes", align_bytes=64)
-        for z, offset in enumerate((4096 - S // 2, 12288)):
-            zeros = early.tile([P, S], U8, name="zeros%d" % z, align_bytes=64, offset=offset)
+        w2_plane = keep.tile([P, N], U8, name="w2_plane", align_bytes=64)
+        for half, offset in enumerate((4096 - N // 4, 17408 - N // 4)):
+            zeros = early.tile([P, N // 2], U8, name="zeros%d" % half, align_bytes=64, offset=offset)
             nc.vector.memset(zeros[:].bitcast(I32), 0)
-            nc.vector.tensor_copy(x_planes[:, z, :].bitcast(I32), zeros[:].bitcast(I32))
+            nc.vector.tensor_copy(
+                w2_plane[:, half * N // 2 : (half + 1) * N // 2].bitcast(I32), zeros[:].bitcast(I32)
+            )
+        for q in range(4):
+            nc.gpsimd.dma_start(
+                out=w2_plane[QUADRANT * q : QUADRANT * q + 4, :].bitcast(I32),
+                in_=w2_scales[0, 4 * q : 4 * q + 4, :].bitcast(I32),
+            )
 
         raw0_vector = load_w1(0, P // 2, P, early, 0)
         table0 = early.tile([P, T], U32, name="table0", align_bytes=64, offset=4096)
         load_words(0, table0)
         raw1_scalar = load_w1(1, 0, SCALAR_M, early, 12288)
+        raw1_vector = load_w1(1, SCALAR_M, P, early, 17408)
 
         picked_scales = reuse.tile([P, S], U8, name="picked_scales", align_bytes=64, offset=0)
         nc.vector.tensor_copy(picked_scales[:], scale_table[:].indirect(offsets[:]))
-        for q in range(4):
-            nc.sync.dma_start(
-                out=x_planes[QUADRANT * q : QUADRANT * q + 4, :, :].bitcast(I32),
-                in_=picked_scales[QUADRANT * q : QUADRANT * (q + 1) : 4, :].bitcast(I32),
-            )
+        x_planes = keep.tile([P, S], U8, name="x_planes", align_bytes=64)
+        nc.vector.tensor_copy(x_planes[:].bitcast(I32), picked_scales[:].bitcast(I32))
+        for r in range(2):
+            for z in range(PASSES):
+                nc.sync.dma_start(
+                    out=x_planes[8 * z + 2 + r : P : QUADRANT, :].bitcast(I32),
+                    in_=picked_scales[16 + 8 * z + r : P : QUADRANT, :].bitcast(I32),
+                )
 
         word_table = [table0]
 
         w1_codes = [keep.tile([P, H], U32, name="w1_codes%d" % z, align_bytes=64) for z in range(PASSES)]
         w1_plane = [keep.tile([P, H], U8, name="w1_plane%d" % z, align_bytes=64) for z in range(PASSES)]
 
-        def quantize_w1(z, split, low, high):
+        def quantize_w1(z, parts):
             grouped = stage.tile([P, PACK, P, PACK], BF16, name="w1_grouped%d" % z, align_bytes=64, offset=4096 * z)
-            for copy, m0, m1, raw in ((nc.scalar.copy, 0, split, low), (nc.vector.tensor_copy, split, P, high)):
+            for copy, m0, m1, raw, first in parts:
                 copy(
                     out=grouped[:, :, m0:m1, :].rearrange("p t m j -> p m t j"),
-                    in_=raw[:].rearrange("p j (m t) -> p m t j", t=PACK),
+                    in_=raw[:].rearrange("p j (m t) -> p m t j", t=PACK)[:, m0 - first : m1 - first],
                 )
             nc.vector.quantize_mx(
                 out=w1_codes[z][:].bitcast(FP8X4),
@@ -95,7 +108,6 @@ def tile_picked_phpool_none_p_kernel(tc, x_words, x_scales, w1, w2_words, w2_sca
                 in_=grouped[:].rearrange("p t m j -> p (t m j)"),
             )
 
-        banks = [psum.tile([P, PACK, CHUNK], F32, name="bank%d" % b, tag="bank%d" % b) for b in range(2 * CHUNKS)]
         starts = [V, 0, V + SLICE, SLICE]
 
         def gather(z, s0):
@@ -113,24 +125,28 @@ def tile_picked_phpool_none_p_kernel(tc, x_words, x_scales, w1, w2_words, w2_sca
                         lhsT=w1_codes[z][:, t * P : (t + 1) * P].bitcast(FP8X4),
                         lhsT_scale=w1_plane[z][:, t * P : (t + 1) * P],
                         rhs=picked[:, c0 : c0 + CHUNK].bitcast(FP8X4),
-                        rhs_scale=x_planes[:, z, s0 + c0 : s0 + c0 + CHUNK],
+                        rhs_scale=x_planes[8 * z :, s0 + c0 : s0 + c0 + CHUNK],
                         start=(z == 0 and t == 0),
                         stop=(z == PASSES - 1 and t == PACK - 1),
                     )
 
-        quantize_w1(0, P // 2, raw0_scalar, raw0_vector)
-        raw1_vector = load_w1(1, SCALAR_M, P, early, 26624)
-        table1 = early.tile([P, T], U32, name="table1", align_bytes=64, offset=18432)
+        quantize_w1(0, [(nc.scalar.copy, 0, P // 2, raw0_scalar, 0), (nc.scalar.copy, P // 2, P, raw0_vector, P // 2)])
+        warm = psum.tile([P, H], F32, name="warm", tag="bank%d" % CHUNKS)
+        for i in range(3):
+            nc.tensor.matmul_mx(
+                out=warm[:],
+                lhsT=w1_codes[0][:, 0:P].bitcast(FP8X4),
+                lhsT_scale=w1_plane[0][:, 0:P],
+                rhs=w1_codes[0][:].bitcast(FP8X4),
+                rhs_scale=w1_plane[0][:],
+                start=True,
+                stop=True,
+            )
+        banks = [psum.tile([P, PACK, CHUNK], F32, name="bank%d" % b, tag="bank%d" % b) for b in range(2 * CHUNKS)]
+        table1 = early.tile([P, T], U32, name="table1", align_bytes=64, offset=20480)
         load_words(1, table1)
         word_table.append(table1)
 
-        w2_plane = reuse.tile([P, N], U8, name="w2_plane", align_bytes=64, offset=0)
-        nc.gpsimd.memset(w2_plane[:].bitcast(I32), 0)
-        for q in range(4):
-            nc.sync.dma_start(
-                out=w2_plane[QUADRANT * q : QUADRANT * q + 4, :].bitcast(I32),
-                in_=w2_scales[0, 4 * q : 4 * q + 4, :].bitcast(I32),
-            )
         w2_codes = reuse.tile([P, N], U32, name="w2_codes", align_bytes=64, offset=N)
         nc.sync.dma_start(
             out=w2_codes[:].bitcast(I32),
@@ -139,7 +155,14 @@ def tile_picked_phpool_none_p_kernel(tc, x_words, x_scales, w1, w2_words, w2_sca
 
         for s0 in starts:
             project(0, s0, gather(0, s0))
-        quantize_w1(1, SCALAR_M, raw1_scalar, raw1_vector)
+        quantize_w1(
+            1,
+            [
+                (nc.scalar.copy, 0, SCALAR_M, raw1_scalar, 0),
+                (nc.scalar.copy, SCALAR_M, VECTOR_M, raw1_vector, SCALAR_M),
+                (nc.vector.tensor_copy, VECTOR_M, P, raw1_vector, SCALAR_M),
+            ],
+        )
         for s0 in starts:
             project(1, s0, gather(1, s0))
 

@@ -21,9 +21,9 @@ QUADRANT = 32
 SLICE = 256
 CHUNK = 128
 CHUNKS = V // CHUNK
-SCALAR_M = 80
+SCALAR_M = 64
 VECTOR_M = 96
-RUN = 4
+RUN = 2
 
 
 def tile_picked_phpool_none_p_kernel(tc, x_words, x_scales, w1, w2_words, w2_scales, offs, out):
@@ -54,41 +54,29 @@ def tile_picked_phpool_none_p_kernel(tc, x_words, x_scales, w1, w2_words, w2_sca
 
         scale_table = keep.tile([P, T], U8, name="scale_table", align_bytes=64)
         nc.vector.memset(scale_table[:].bitcast(I32), 0)
-        for r in range(2):
-            nc.sync.dma_start(
-                out=scale_table[r:P:8, :].bitcast(I32),
-                in_=x_scales.rearrange("z (g r) c -> r g z c", r=2)[r].bitcast(I32),
-            )
+        nc.sync.dma_start(
+            out=scale_table[0:P:4, :].bitcast(I32),
+            in_=x_scales.rearrange("z q c -> q z c").bitcast(I32),
+        )
 
-        w2_plane = keep.tile([P, N], U8, name="w2_plane", align_bytes=64)
-        for half, offset in enumerate((4096 - N // 4, 17408 - N // 4)):
-            zeros = early.tile([P, N // 2], U8, name="zeros%d" % half, align_bytes=64, offset=offset)
+        x_planes = keep.tile([P, PASSES, S], U8, name="x_planes", align_bytes=64)
+        for z, offset in enumerate((4096 - S // 2, 12288)):
+            zeros = early.tile([P, S], U8, name="zeros%d" % z, align_bytes=64, offset=offset)
             nc.vector.memset(zeros[:].bitcast(I32), 0)
-            nc.vector.tensor_copy(
-                w2_plane[:, half * N // 2 : (half + 1) * N // 2].bitcast(I32), zeros[:].bitcast(I32)
-            )
-        for q in range(4):
-            nc.gpsimd.dma_start(
-                out=w2_plane[QUADRANT * q : QUADRANT * q + 4, :].bitcast(I32),
-                in_=w2_scales[0, 4 * q : 4 * q + 4, :].bitcast(I32),
-            )
+            nc.vector.tensor_copy(x_planes[:, z, :].bitcast(I32), zeros[:].bitcast(I32))
 
         raw0_vector = load_w1(0, P // 2, P, early, 0)
         table0 = early.tile([P, T], U32, name="table0", align_bytes=64, offset=4096)
         load_words(0, table0)
         raw1_scalar = load_w1(1, 0, SCALAR_M, early, 12288)
-        raw1_vector = load_w1(1, SCALAR_M, P, early, 17408)
 
         picked_scales = reuse.tile([P, S], U8, name="picked_scales", align_bytes=64, offset=0)
         nc.vector.tensor_copy(picked_scales[:], scale_table[:].indirect(offsets[:]))
-        x_planes = keep.tile([P, S], U8, name="x_planes", align_bytes=64)
-        nc.vector.tensor_copy(x_planes[:].bitcast(I32), picked_scales[:].bitcast(I32))
-        for r in range(2):
-            for z in range(PASSES):
-                nc.sync.dma_start(
-                    out=x_planes[8 * z + 2 + r : P : QUADRANT, :].bitcast(I32),
-                    in_=picked_scales[16 + 8 * z + r : P : QUADRANT, :].bitcast(I32),
-                )
+        for q in range(4):
+            nc.sync.dma_start(
+                out=x_planes[QUADRANT * q : QUADRANT * q + 4, :, :].bitcast(I32),
+                in_=picked_scales[QUADRANT * q : QUADRANT * (q + 1) : 4, :].bitcast(I32),
+            )
 
         word_table = [table0]
 
@@ -125,7 +113,7 @@ def tile_picked_phpool_none_p_kernel(tc, x_words, x_scales, w1, w2_words, w2_sca
                         lhsT=w1_codes[z][:, t * P : (t + 1) * P].bitcast(FP8X4),
                         lhsT_scale=w1_plane[z][:, t * P : (t + 1) * P],
                         rhs=picked[:, c0 : c0 + CHUNK].bitcast(FP8X4),
-                        rhs_scale=x_planes[8 * z :, s0 + c0 : s0 + c0 + CHUNK],
+                        rhs_scale=x_planes[:, z, s0 + c0 : s0 + c0 + CHUNK],
                         start=(z == 0 and t == 0),
                         stop=(z == PASSES - 1 and t == PACK - 1),
                     )
@@ -143,10 +131,18 @@ def tile_picked_phpool_none_p_kernel(tc, x_words, x_scales, w1, w2_words, w2_sca
                 stop=True,
             )
         banks = [psum.tile([P, PACK, CHUNK], F32, name="bank%d" % b, tag="bank%d" % b) for b in range(2 * CHUNKS)]
-        table1 = early.tile([P, T], U32, name="table1", align_bytes=64, offset=20480)
+        raw1_vector = load_w1(1, SCALAR_M, P, early, 26624)
+        table1 = early.tile([P, T], U32, name="table1", align_bytes=64, offset=18432)
         load_words(1, table1)
         word_table.append(table1)
 
+        w2_plane = reuse.tile([P, N], U8, name="w2_plane", align_bytes=64, offset=0)
+        nc.gpsimd.memset(w2_plane[:].bitcast(I32), 0)
+        for q in range(4):
+            nc.sync.dma_start(
+                out=w2_plane[QUADRANT * q : QUADRANT * q + 4, :].bitcast(I32),
+                in_=w2_scales[0, 4 * q : 4 * q + 4, :].bitcast(I32),
+            )
         w2_codes = reuse.tile([P, N], U32, name="w2_codes", align_bytes=64, offset=N)
         nc.sync.dma_start(
             out=w2_codes[:].bitcast(I32),
@@ -187,29 +183,30 @@ def tile_picked_phpool_none_p_kernel(tc, x_words, x_scales, w1, w2_words, w2_sca
         firsts = [walk_bank(c) for c in range(CHUNKS - 1)] + [rounded_in_word_order(CHUNKS - 1)]
 
         out_view = out.rearrange("(h p) v -> p h v", p=P)
-        groups = [(0, 2), (2, 3), (3, 4)]
-        for g, (c0, c1) in enumerate(groups):
-            width = (c1 - c0) * CHUNK
-            cols = slice(c0 * CHUNK, c1 * CHUNK)
-            z_grouped = reuse.tile(
-                [P, width, PACK], BF16, name="z_grouped%d" % g, align_bytes=64, offset=(2048, 2048, 4096)[g]
+        z_grouped = [keep.tile([P, CHUNK, PACK], BF16, name="z_grouped%d" % c, align_bytes=64) for c in range(CHUNKS)]
+
+        def larger(c):
+            nc.vector.tensor_tensor(
+                out=walk_words(z_grouped[c][:]) if c < CHUNKS - 1 else z_grouped[c][:],
+                in0=firsts[c],
+                in1=seconds[c],
+                op=mybir.AluOpType.max,
             )
-            for c in range(c0, c1):
-                z_chunk = z_grouped[:, (c - c0) * CHUNK : (c - c0 + 1) * CHUNK, :]
-                nc.vector.tensor_tensor(
-                    out=walk_words(z_chunk) if c < CHUNKS - 1 else z_chunk,
-                    in0=firsts[c],
-                    in1=seconds[c],
-                    op=mybir.AluOpType.max,
+
+        def second_layer(c):
+            if c < 2:
+                z_codes = stage.tile(
+                    [P, CHUNK], U32, name="z_codes%d" % c, align_bytes=64, offset=4096 + 4 * (V + SLICE, SLICE)[c]
                 )
-            z_codes = keep.tile([P, width], U32, name="z_codes%d" % g, align_bytes=64)
-            z_plane = keep.tile([P, width], U8, name="z_plane%d" % g, align_bytes=64)
+            else:
+                z_codes = keep.tile([P, CHUNK], U32, name="z_codes%d" % c, align_bytes=64)
+            z_plane = keep.tile([P, CHUNK], U8, name="z_plane%d" % c, align_bytes=64)
             nc.vector.quantize_mx(
-                out=z_codes[:].bitcast(FP8X4), scales=z_plane[:], in_=z_grouped[:].rearrange("p v t -> p (v t)")
+                out=z_codes[:].bitcast(FP8X4), scales=z_plane[:], in_=z_grouped[c][:].rearrange("p v t -> p (v t)")
             )
-            last = g == len(groups) - 1
+            last = c == CHUNKS - 1
             accs = [
-                psum.tile([P, N // P, width], F32, name="acc%d_%d" % (g, b), tag="bank%d" % (CHUNKS + c0 - CHUNKS * b))
+                psum.tile([P, N // P, CHUNK], F32, name="acc%d_%d" % (c, b), tag="bank%d" % (CHUNKS + c - CHUNKS * b))
                 for b in range(2 if last else 1)
             ]
             for h in range(N // P):
@@ -222,10 +219,16 @@ def tile_picked_phpool_none_p_kernel(tc, x_words, x_scales, w1, w2_words, w2_sca
                     start=True,
                     stop=True,
                 )
-            result = keep.tile([P, N // P, width], F32, name="result%d" % g, align_bytes=64)
+            result = keep.tile([P, N // P, CHUNK], F32, name="result%d" % c, align_bytes=64)
             if last:
                 nc.scalar.copy(out=result[:, 0, :], in_=accs[0][:, 0, :])
                 nc.vector.tensor_copy(out=result[:, 1, :], in_=accs[1][:, 1, :])
             else:
                 nc.scalar.copy(out=result[:], in_=accs[0][:])
-            nc.sync.dma_start(out=out_view[:, :, cols], in_=result[:])
+            nc.sync.dma_start(out=out_view[:, :, c * CHUNK : (c + 1) * CHUNK], in_=result[:])
+
+        larger(0)
+        for c in range(1, CHUNKS):
+            larger(c)
+            second_layer(c - 1)
+        second_layer(CHUNKS - 1)

@@ -59,11 +59,11 @@ def tile_picked_phpool_none_p_kernel(tc, x_words, x_scales, w1, w2_words, w2_sca
             in_=x_scales.rearrange("z q c -> q z c").bitcast(I32),
         )
 
-        x_planes = keep.tile([P, PASSES, S], U8, name="x_planes", align_bytes=64)
-        for z, offset in enumerate((4096 - S // 2, 12288)):
-            zeros = early.tile([P, S], U8, name="zeros%d" % z, align_bytes=64, offset=offset)
+        x_planes = [keep.tile([P, S], U8, name="x_plane0", align_bytes=64)]
+        for half, offset in enumerate((4096 - V // 2, 12288)):
+            zeros = early.tile([P, V], U8, name="zeros%d" % half, align_bytes=64, offset=offset)
             nc.vector.memset(zeros[:].bitcast(I32), 0)
-            nc.vector.tensor_copy(x_planes[:, z, :].bitcast(I32), zeros[:].bitcast(I32))
+            nc.vector.tensor_copy(x_planes[0][:, half * V : (half + 1) * V].bitcast(I32), zeros[:].bitcast(I32))
 
         raw0_vector = load_w1(0, P // 2, P, early, 0)
         table0 = early.tile([P, T], U32, name="table0", align_bytes=64, offset=4096)
@@ -72,11 +72,15 @@ def tile_picked_phpool_none_p_kernel(tc, x_words, x_scales, w1, w2_words, w2_sca
 
         picked_scales = reuse.tile([P, S], U8, name="picked_scales", align_bytes=64, offset=0)
         nc.vector.tensor_copy(picked_scales[:], scale_table[:].indirect(offsets[:]))
-        for q in range(4):
-            nc.sync.dma_start(
-                out=x_planes[QUADRANT * q : QUADRANT * q + 4, :, :].bitcast(I32),
-                in_=picked_scales[QUADRANT * q : QUADRANT * (q + 1) : 4, :].bitcast(I32),
-            )
+
+        def move_scale_rows(z):
+            for r in range(4):
+                nc.sync.dma_start(
+                    out=x_planes[z][r:P:QUADRANT, :].bitcast(I32),
+                    in_=picked_scales[8 * r + 4 * z : P : QUADRANT, :].bitcast(I32),
+                )
+
+        move_scale_rows(0)
 
         word_table = [table0]
 
@@ -113,37 +117,29 @@ def tile_picked_phpool_none_p_kernel(tc, x_words, x_scales, w1, w2_words, w2_sca
                         lhsT=w1_codes[z][:, t * P : (t + 1) * P].bitcast(FP8X4),
                         lhsT_scale=w1_plane[z][:, t * P : (t + 1) * P],
                         rhs=picked[:, c0 : c0 + CHUNK].bitcast(FP8X4),
-                        rhs_scale=x_planes[:, z, s0 + c0 : s0 + c0 + CHUNK],
+                        rhs_scale=x_planes[z][:, s0 + c0 : s0 + c0 + CHUNK],
                         start=(z == 0 and t == 0),
                         stop=(z == PASSES - 1 and t == PACK - 1),
                     )
 
         quantize_w1(0, [(nc.scalar.copy, 0, P // 2, raw0_scalar, 0), (nc.scalar.copy, P // 2, P, raw0_vector, P // 2)])
-        warm = psum.tile([P, H], F32, name="warm", tag="bank%d" % CHUNKS)
-        for i in range(3):
-            nc.tensor.matmul_mx(
-                out=warm[:],
-                lhsT=w1_codes[0][:, 0:P].bitcast(FP8X4),
-                lhsT_scale=w1_plane[0][:, 0:P],
-                rhs=w1_codes[0][:].bitcast(FP8X4),
-                rhs_scale=w1_plane[0][:],
-                start=True,
-                stop=True,
-            )
         banks = [psum.tile([P, PACK, CHUNK], F32, name="bank%d" % b, tag="bank%d" % b) for b in range(2 * CHUNKS)]
         raw1_vector = load_w1(1, SCALAR_M, P, early, 26624)
         table1 = early.tile([P, T], U32, name="table1", align_bytes=64, offset=18432)
         load_words(1, table1)
         word_table.append(table1)
+        x_planes.append(early.tile([P, S], U8, name="x_plane1", align_bytes=64, offset=0))
+        nc.vector.memset(x_planes[1][:].bitcast(I32), 0)
+        move_scale_rows(1)
 
-        w2_plane = reuse.tile([P, N], U8, name="w2_plane", align_bytes=64, offset=0)
+        w2_plane = early.tile([P, N], U8, name="w2_plane", align_bytes=64, offset=12288)
         nc.gpsimd.memset(w2_plane[:].bitcast(I32), 0)
         for q in range(4):
             nc.sync.dma_start(
                 out=w2_plane[QUADRANT * q : QUADRANT * q + 4, :].bitcast(I32),
                 in_=w2_scales[0, 4 * q : 4 * q + 4, :].bitcast(I32),
             )
-        w2_codes = reuse.tile([P, N], U32, name="w2_codes", align_bytes=64, offset=N)
+        w2_codes = early.tile([P, N], U32, name="w2_codes", align_bytes=64, offset=12288 + N)
         nc.sync.dma_start(
             out=w2_codes[:].bitcast(I32),
             in_=w2_words[0].rearrange("p n t -> p (n t)").bitcast(I32),

@@ -21,8 +21,7 @@ QUADRANT = 32
 SLICE = 256
 CHUNK = 128
 CHUNKS = V // CHUNK
-SCALAR_M = 64
-VECTOR_M = 96
+SCALAR_M = 56
 RUN = 2
 
 
@@ -68,7 +67,7 @@ def tile_picked_phpool_none_p_kernel(tc, x_words, x_scales, w1, w2_words, w2_sca
         raw0_vector = load_w1(0, P // 2, P, early, 0)
         table0 = early.tile([P, T], U32, name="table0", align_bytes=64, offset=4096)
         load_words(0, table0)
-        raw1_scalar = load_w1(1, 0, SCALAR_M, early, 12288)
+        raw1 = load_w1(1, 0, P, early, 12288)
 
         picked_scales = reuse.tile([P, S], U8, name="picked_scales", align_bytes=64, offset=0)
         nc.vector.tensor_copy(picked_scales[:], scale_table[:].indirect(offsets[:]))
@@ -123,9 +122,19 @@ def tile_picked_phpool_none_p_kernel(tc, x_words, x_scales, w1, w2_words, w2_sca
                     )
 
         quantize_w1(0, [(nc.scalar.copy, 0, P // 2, raw0_scalar, 0), (nc.scalar.copy, P // 2, P, raw0_vector, P // 2)])
+        warm = psum.tile([P, H], F32, name="warm", tag="bank%d" % CHUNKS)
+        for i in range(3):
+            nc.tensor.matmul_mx(
+                out=warm[:],
+                lhsT=w1_codes[0][:, 0:P].bitcast(FP8X4),
+                lhsT_scale=w1_plane[0][:, 0:P],
+                rhs=w1_codes[0][:].bitcast(FP8X4),
+                rhs_scale=w1_plane[0][:],
+                start=True,
+                stop=True,
+            )
         banks = [psum.tile([P, PACK, CHUNK], F32, name="bank%d" % b, tag="bank%d" % b) for b in range(2 * CHUNKS)]
-        raw1_vector = load_w1(1, SCALAR_M, P, early, 26624)
-        table1 = early.tile([P, T], U32, name="table1", align_bytes=64, offset=18432)
+        table1 = early.tile([P, T], U32, name="table1", align_bytes=64, offset=20480)
         load_words(1, table1)
         word_table.append(table1)
         x_planes.append(early.tile([P, S], U8, name="x_plane1", align_bytes=64, offset=0))
@@ -150,9 +159,8 @@ def tile_picked_phpool_none_p_kernel(tc, x_words, x_scales, w1, w2_words, w2_sca
         quantize_w1(
             1,
             [
-                (nc.scalar.copy, 0, SCALAR_M, raw1_scalar, 0),
-                (nc.scalar.copy, SCALAR_M, VECTOR_M, raw1_vector, SCALAR_M),
-                (nc.vector.tensor_copy, VECTOR_M, P, raw1_vector, SCALAR_M),
+                (nc.scalar.copy, 0, SCALAR_M, raw1, 0),
+                (nc.vector.tensor_copy, SCALAR_M, P, raw1, 0),
             ],
         )
         for s0 in starts:

@@ -51,6 +51,11 @@ def tile_picked_phpool_none_p_kernel(tc, x_words, x_scales, w1, w2_words, w2_sca
         offsets = keep.tile([P, S // 16], U16, name="offsets")
         nc.sync.dma_start(offsets[:], offs)
 
+        zeros = [
+            early.tile([P, V], U8, name="zeros%d" % half, align_bytes=64, offset=offset)
+            for half, offset in enumerate((4096 - V // 2, 12288))
+        ]
+        nc.vector.memset(zeros[0][:].bitcast(I32), 0)
         scale_table = keep.tile([P, T], U8, name="scale_table", align_bytes=64)
         nc.vector.memset(scale_table[:].bitcast(I32), 0)
         nc.sync.dma_start(
@@ -59,10 +64,9 @@ def tile_picked_phpool_none_p_kernel(tc, x_words, x_scales, w1, w2_words, w2_sca
         )
 
         x_planes = [keep.tile([P, S], U8, name="x_plane0", align_bytes=64)]
-        for half, offset in enumerate((4096 - V // 2, 12288)):
-            zeros = early.tile([P, V], U8, name="zeros%d" % half, align_bytes=64, offset=offset)
-            nc.vector.memset(zeros[:].bitcast(I32), 0)
-            nc.vector.tensor_copy(x_planes[0][:, half * V : (half + 1) * V].bitcast(I32), zeros[:].bitcast(I32))
+        nc.vector.tensor_copy(x_planes[0][:, 0:V].bitcast(I32), zeros[0][:].bitcast(I32))
+        nc.vector.memset(zeros[1][:].bitcast(I32), 0)
+        nc.vector.tensor_copy(x_planes[0][:, V:S].bitcast(I32), zeros[1][:].bitcast(I32))
 
         raw0_vector = load_w1(0, P // 2, P, early, 0)
         table0 = early.tile([P, T], U32, name="table0", align_bytes=64, offset=4096)
@@ -142,7 +146,7 @@ def tile_picked_phpool_none_p_kernel(tc, x_words, x_scales, w1, w2_words, w2_sca
         move_scale_rows(1)
 
         w2_plane = early.tile([P, N], U8, name="w2_plane", align_bytes=64, offset=12288)
-        nc.gpsimd.memset(w2_plane[:].bitcast(I32), 0)
+        nc.vector.memset(w2_plane[:].bitcast(I32), 0)
         for q in range(4):
             nc.sync.dma_start(
                 out=w2_plane[QUADRANT * q : QUADRANT * q + 4, :].bitcast(I32),
@@ -187,35 +191,45 @@ def tile_picked_phpool_none_p_kernel(tc, x_words, x_scales, w1, w2_words, w2_sca
         firsts = [walk_bank(c) for c in range(CHUNKS - 1)] + [rounded_in_word_order(CHUNKS - 1)]
 
         out_view = out.rearrange("(h p) v -> p h v", p=P)
-        z_grouped = [keep.tile([P, CHUNK, PACK], BF16, name="z_grouped%d" % c, align_bytes=64) for c in range(CHUNKS)]
+        pieces = [(0, 128), (128, 256), (256, 384), (384, 448), (448, 512)]
+        z_grouped = [
+            keep.tile([P, v1 - v0, PACK], BF16, name="z_grouped%d" % v0, align_bytes=64) for v0, v1 in pieces
+        ]
+        results = [
+            keep.tile([P, N // P, width], F32, name="result%d" % i, align_bytes=64)
+            for i, width in enumerate((128, 128, 128, 128))
+        ]
 
-        def larger(c):
-            nc.vector.tensor_tensor(
-                out=walk_words(z_grouped[c][:]) if c < CHUNKS - 1 else z_grouped[c][:],
-                in0=firsts[c],
-                in1=seconds[c],
-                op=mybir.AluOpType.max,
-            )
-
-        def second_layer(c):
-            if c < 2:
-                z_codes = stage.tile(
-                    [P, CHUNK], U32, name="z_codes%d" % c, align_bytes=64, offset=4096 + 4 * (V + SLICE, SLICE)[c]
+        def larger(i):
+            v0, v1 = pieces[i]
+            c = v0 // CHUNK
+            if c < CHUNKS - 1:
+                nc.vector.tensor_tensor(
+                    out=walk_words(z_grouped[i][:]), in0=firsts[c], in1=seconds[c], op=mybir.AluOpType.max
                 )
             else:
-                z_codes = keep.tile([P, CHUNK], U32, name="z_codes%d" % c, align_bytes=64)
-            z_plane = keep.tile([P, CHUNK], U8, name="z_plane%d" % c, align_bytes=64)
+                part = slice(v0 - c * CHUNK, v1 - c * CHUNK)
+                nc.vector.tensor_tensor(
+                    out=z_grouped[i][:], in0=firsts[c][:, part, :], in1=seconds[c][:, part, :], op=mybir.AluOpType.max
+                )
+
+        def second_layer(i):
+            v0, v1 = pieces[i]
+            width = v1 - v0
+            if i < 2:
+                z_codes = stage.tile(
+                    [P, width], U32, name="z_codes%d" % i, align_bytes=64, offset=4096 + 4 * (V + SLICE, SLICE)[i]
+                )
+            else:
+                z_codes = keep.tile([P, width], U32, name="z_codes%d" % i, align_bytes=64)
+            z_plane = keep.tile([P, width], U8, name="z_plane%d" % i, align_bytes=64)
             nc.vector.quantize_mx(
-                out=z_codes[:].bitcast(FP8X4), scales=z_plane[:], in_=z_grouped[c][:].rearrange("p v t -> p (v t)")
+                out=z_codes[:].bitcast(FP8X4), scales=z_plane[:], in_=z_grouped[i][:].rearrange("p v t -> p (v t)")
             )
-            last = c == CHUNKS - 1
-            accs = [
-                psum.tile([P, N // P, CHUNK], F32, name="acc%d_%d" % (c, b), tag="bank%d" % (CHUNKS + c - CHUNKS * b))
-                for b in range(2 if last else 1)
-            ]
+            acc = psum.tile([P, N // P, width], F32, name="acc%d" % i, tag="bank%d" % (4, 5, 6, 7, 3)[i])
             for h in range(N // P):
                 nc.tensor.matmul_mx(
-                    out=accs[h if last else 0][:, h, :],
+                    out=acc[:, h, :],
                     lhsT=w2_codes[:, h * P : (h + 1) * P].bitcast(FP8X4),
                     lhsT_scale=w2_plane[:, h * P : (h + 1) * P],
                     rhs=z_codes[:].bitcast(FP8X4),
@@ -223,16 +237,18 @@ def tile_picked_phpool_none_p_kernel(tc, x_words, x_scales, w1, w2_words, w2_sca
                     start=True,
                     stop=True,
                 )
-            result = keep.tile([P, N // P, CHUNK], F32, name="result%d" % c, align_bytes=64)
-            if last:
-                nc.scalar.copy(out=result[:, 0, :], in_=accs[0][:, 0, :])
-                nc.vector.tensor_copy(out=result[:, 1, :], in_=accs[1][:, 1, :])
-            else:
-                nc.scalar.copy(out=result[:], in_=accs[0][:])
-            nc.sync.dma_start(out=out_view[:, :, c * CHUNK : (c + 1) * CHUNK], in_=result[:])
+            c = v0 // CHUNK
+            copy = nc.vector.tensor_copy if i == len(pieces) - 1 else nc.scalar.copy
+            copy(out=results[c][:, :, v0 - c * CHUNK : v1 - c * CHUNK], in_=acc[:])
+            if v1 % CHUNK == 0:
+                nc.sync.dma_start(out=out_view[:, :, c * CHUNK : v1], in_=results[c][:])
 
         larger(0)
-        for c in range(1, CHUNKS):
-            larger(c)
-            second_layer(c - 1)
-        second_layer(CHUNKS - 1)
+        larger(1)
+        second_layer(0)
+        larger(2)
+        second_layer(1)
+        larger(3)
+        larger(4)
+        for i in range(2, len(pieces)):
+            second_layer(i)

@@ -21,7 +21,7 @@ QUADRANT = 32
 SLICE = 256
 CHUNK = 128
 CHUNKS = V // CHUNK
-SCALAR_M = 56
+SCALAR_M = 48
 RUN = 2
 
 
@@ -107,7 +107,7 @@ def tile_picked_phpool_none_p_kernel(tc, x_words, x_scales, w1, w2_words, w2_sca
 
         def gather(z, s0):
             picked = stage.tile(
-                [P, SLICE], U32, name="picked%d_%d" % (z, s0), align_bytes=64, offset=4096 * z + 4 * s0
+                [P, SLICE], U32, name="picked%d_%d" % (z, s0), align_bytes=64, offset=8192 + 4096 * z + 4 * s0
             )
             nc.vector.tensor_copy(picked[:], word_table[z][:].indirect(offsets[:, s0 // 16 : (s0 + SLICE) // 16]))
             return picked
@@ -191,45 +191,35 @@ def tile_picked_phpool_none_p_kernel(tc, x_words, x_scales, w1, w2_words, w2_sca
         firsts = [walk_bank(c) for c in range(CHUNKS - 1)] + [rounded_in_word_order(CHUNKS - 1)]
 
         out_view = out.rearrange("(h p) v -> p h v", p=P)
-        pieces = [(0, 128), (128, 256), (256, 384), (384, 448), (448, 512)]
-        z_grouped = [
-            keep.tile([P, v1 - v0, PACK], BF16, name="z_grouped%d" % v0, align_bytes=64) for v0, v1 in pieces
-        ]
-        results = [
-            keep.tile([P, N // P, width], F32, name="result%d" % i, align_bytes=64)
-            for i, width in enumerate((128, 128, 128, 128))
-        ]
+        z_grouped = [keep.tile([P, CHUNK, PACK], BF16, name="z_grouped%d" % c, align_bytes=64) for c in range(CHUNKS)]
 
-        def larger(i):
-            v0, v1 = pieces[i]
-            c = v0 // CHUNK
-            if c < CHUNKS - 1:
-                nc.vector.tensor_tensor(
-                    out=walk_words(z_grouped[i][:]), in0=firsts[c], in1=seconds[c], op=mybir.AluOpType.max
-                )
-            else:
-                part = slice(v0 - c * CHUNK, v1 - c * CHUNK)
-                nc.vector.tensor_tensor(
-                    out=z_grouped[i][:], in0=firsts[c][:, part, :], in1=seconds[c][:, part, :], op=mybir.AluOpType.max
-                )
-
-        def second_layer(i):
-            v0, v1 = pieces[i]
-            width = v1 - v0
-            if i < 2:
-                z_codes = stage.tile(
-                    [P, width], U32, name="z_codes%d" % i, align_bytes=64, offset=4096 + 4 * (V + SLICE, SLICE)[i]
-                )
-            else:
-                z_codes = keep.tile([P, width], U32, name="z_codes%d" % i, align_bytes=64)
-            z_plane = keep.tile([P, width], U8, name="z_plane%d" % i, align_bytes=64)
-            nc.vector.quantize_mx(
-                out=z_codes[:].bitcast(FP8X4), scales=z_plane[:], in_=z_grouped[i][:].rearrange("p v t -> p (v t)")
+        def larger(c):
+            nc.vector.tensor_tensor(
+                out=walk_words(z_grouped[c][:]) if c < CHUNKS - 1 else z_grouped[c][:],
+                in0=firsts[c],
+                in1=seconds[c],
+                op=mybir.AluOpType.max,
             )
-            acc = psum.tile([P, N // P, width], F32, name="acc%d" % i, tag="bank%d" % (4, 5, 6, 7, 3)[i])
+
+        def second_layer(c):
+            if c < 2:
+                z_codes = stage.tile(
+                    [P, CHUNK], U32, name="z_codes%d" % c, align_bytes=64, offset=12288 + 4 * (V + SLICE, SLICE)[c]
+                )
+            else:
+                z_codes = keep.tile([P, CHUNK], U32, name="z_codes%d" % c, align_bytes=64)
+            z_plane = keep.tile([P, CHUNK], U8, name="z_plane%d" % c, align_bytes=64)
+            nc.vector.quantize_mx(
+                out=z_codes[:].bitcast(FP8X4), scales=z_plane[:], in_=z_grouped[c][:].rearrange("p v t -> p (v t)")
+            )
+            last = c == CHUNKS - 1
+            accs = [
+                psum.tile([P, N // P, CHUNK], F32, name="acc%d_%d" % (c, b), tag="bank%d" % (CHUNKS + c - CHUNKS * b))
+                for b in range(2 if last else 1)
+            ]
             for h in range(N // P):
                 nc.tensor.matmul_mx(
-                    out=acc[:, h, :],
+                    out=accs[h if last else 0][:, h, :],
                     lhsT=w2_codes[:, h * P : (h + 1) * P].bitcast(FP8X4),
                     lhsT_scale=w2_plane[:, h * P : (h + 1) * P],
                     rhs=z_codes[:].bitcast(FP8X4),
@@ -237,18 +227,16 @@ def tile_picked_phpool_none_p_kernel(tc, x_words, x_scales, w1, w2_words, w2_sca
                     start=True,
                     stop=True,
                 )
-            c = v0 // CHUNK
-            copy = nc.vector.tensor_copy if i == len(pieces) - 1 else nc.scalar.copy
-            copy(out=results[c][:, :, v0 - c * CHUNK : v1 - c * CHUNK], in_=acc[:])
-            if v1 % CHUNK == 0:
-                nc.sync.dma_start(out=out_view[:, :, c * CHUNK : v1], in_=results[c][:])
+            result = keep.tile([P, N // P, CHUNK], F32, name="result%d" % c, align_bytes=64)
+            if last:
+                nc.scalar.copy(out=result[:, 0, :], in_=accs[0][:, 0, :])
+                nc.vector.tensor_copy(out=result[:, 1, :], in_=accs[1][:, 1, :])
+            else:
+                nc.scalar.copy(out=result[:], in_=accs[0][:])
+            nc.sync.dma_start(out=out_view[:, :, c * CHUNK : (c + 1) * CHUNK], in_=result[:])
 
         larger(0)
-        larger(1)
-        second_layer(0)
-        larger(2)
-        second_layer(1)
-        larger(3)
-        larger(4)
-        for i in range(2, len(pieces)):
-            second_layer(i)
+        for c in range(1, CHUNKS):
+            larger(c)
+            second_layer(c - 1)
+        second_layer(CHUNKS - 1)

@@ -126,17 +126,6 @@ def tile_picked_phpool_none_p_kernel(tc, x_words, x_scales, w1, w2_words, w2_sca
                     )
 
         quantize_w1(0, [(nc.scalar.copy, 0, P // 2, raw0_scalar, 0), (nc.scalar.copy, P // 2, P, raw0_vector, P // 2)])
-        warm = psum.tile([P, H], F32, name="warm", tag="bank%d" % CHUNKS)
-        for i in range(3):
-            nc.tensor.matmul_mx(
-                out=warm[:],
-                lhsT=w1_codes[0][:, 0:P].bitcast(FP8X4),
-                lhsT_scale=w1_plane[0][:, 0:P],
-                rhs=w1_codes[0][:].bitcast(FP8X4),
-                rhs_scale=w1_plane[0][:],
-                start=True,
-                stop=True,
-            )
         banks = [psum.tile([P, PACK, CHUNK], F32, name="bank%d" % b, tag="bank%d" % b) for b in range(2 * CHUNKS)]
         table1 = early.tile([P, T], U32, name="table1", align_bytes=64, offset=20480)
         load_words(1, table1)

@@ -21,7 +21,7 @@ QUADRANT = 32
 SLICE = 256
 CHUNK = 128
 CHUNKS = V // CHUNK
-SCALAR_M = 48
+SCALAR_M = 72
 RUN = 2
 
 
@@ -46,7 +46,13 @@ def tile_picked_phpool_none_p_kernel(tc, x_words, x_scales, w1, w2_words, w2_sca
             nc.sync.dma_start(out=raw[:], in_=rows.rearrange("(p j) c -> p j c", j=PACK))
             return raw
 
-        raw0_scalar = load_w1(0, 0, P // 2, early, 25600)
+        def load_row_pairs(h, offset):
+            raw = early.tile([P, 2, H], F32, name="raw0_pair%d" % h, align_bytes=64, offset=offset)
+            rows = w1[0:K_PASS, :].rearrange("(p j) c -> p j c", j=PACK)
+            nc.sync.dma_start(out=raw[:], in_=rows[:, 2 * h : 2 * h + 2, :])
+            return raw
+
+        raw0_scalar = load_row_pairs(0, 25600)
 
         offsets = keep.tile([P, S // 16], U16, name="offsets")
         nc.sync.dma_start(offsets[:], offs)
@@ -68,7 +74,7 @@ def tile_picked_phpool_none_p_kernel(tc, x_words, x_scales, w1, w2_words, w2_sca
         nc.vector.memset(zeros[1][:].bitcast(I32), 0)
         nc.vector.tensor_copy(x_planes[0][:, V:S].bitcast(I32), zeros[1][:].bitcast(I32))
 
-        raw0_vector = load_w1(0, P // 2, P, early, 0)
+        raw0_vector = load_row_pairs(1, 0)
         table0 = early.tile([P, T], U32, name="table0", align_bytes=64, offset=4096)
         load_words(0, table0)
         raw1 = load_w1(1, 0, P, early, 12288)
@@ -125,7 +131,19 @@ def tile_picked_phpool_none_p_kernel(tc, x_words, x_scales, w1, w2_words, w2_sca
                         stop=(z == PASSES - 1 and t == PACK - 1),
                     )
 
-        quantize_w1(0, [(nc.scalar.copy, 0, P // 2, raw0_scalar, 0), (nc.scalar.copy, P // 2, P, raw0_vector, P // 2)])
+        pairs = keep.tile([P, 2, PACK, P, 2], BF16, name="pairs", align_bytes=64)
+        for h, raw in enumerate((raw0_scalar, raw0_vector)):
+            nc.scalar.copy(
+                out=pairs[:, h].rearrange("p t m j -> p m t j"),
+                in_=raw[:].rearrange("p j (m t) -> p m t j", t=PACK),
+            )
+        grouped0 = stage.tile([P, H, 2, 2], BF16, name="grouped0", align_bytes=64, offset=0)
+        nc.vector.tensor_copy(out=grouped0[:], in_=pairs[:].rearrange("p h t m j -> p (t m) h j"))
+        nc.vector.quantize_mx(
+            out=w1_codes[0][:].bitcast(FP8X4),
+            scales=w1_plane[0][:],
+            in_=grouped0[:].rearrange("p c h j -> p (c h j)"),
+        )
         banks = [psum.tile([P, PACK, CHUNK], F32, name="bank%d" % b, tag="bank%d" % b) for b in range(2 * CHUNKS)]
         table1 = early.tile([P, T], U32, name="table1", align_bytes=64, offset=20480)
         load_words(1, table1)

@@ -93,7 +93,10 @@ def tile_picked_phpool_none_p_kernel(tc, x_words, x_scales, w1, w2_words, w2_sca
 
         word_table = [table0]
 
-        w1_codes = [keep.tile([P, H], U32, name="w1_codes%d" % z, align_bytes=64) for z in range(PASSES)]
+        w1_codes = [
+            early.tile([P, H], U32, name="w1_codes0", align_bytes=64, offset=1024),
+            keep.tile([P, H], U32, name="w1_codes1", align_bytes=64),
+        ]
         w1_plane = [keep.tile([P, H], U8, name="w1_plane%d" % z, align_bytes=64) for z in range(PASSES)]
 
         def quantize_w1(z, parts):
@@ -131,25 +134,45 @@ def tile_picked_phpool_none_p_kernel(tc, x_words, x_scales, w1, w2_words, w2_sca
                         stop=(z == PASSES - 1 and t == PACK - 1),
                     )
 
-        pairs = keep.tile([P, 2, PACK, P, 2], BF16, name="pairs", align_bytes=64)
-        for h, raw in enumerate((raw0_scalar, raw0_vector)):
+        pairs = [keep.tile([P, 2, 2, P, 2], BF16, name="pairs%d" % u, align_bytes=64) for u in range(2)]
+
+        def round_pairs(h, raw, u):
             nc.scalar.copy(
-                out=pairs[:, h].rearrange("p t m j -> p m t j"),
-                in_=raw[:].rearrange("p j (m t) -> p m t j", t=PACK),
+                out=pairs[u][:, h].rearrange("p t m j -> p m t j"),
+                in_=raw[:].rearrange("p j (m t) -> p m t j", t=PACK)[:, :, 2 * u : 2 * u + 2],
             )
-        grouped0 = stage.tile([P, H, 2, 2], BF16, name="grouped0", align_bytes=64, offset=0)
-        nc.vector.tensor_copy(out=grouped0[:], in_=pairs[:].rearrange("p h t m j -> p (t m) h j"))
-        nc.vector.quantize_mx(
-            out=w1_codes[0][:].bitcast(FP8X4),
-            scales=w1_plane[0][:],
-            in_=grouped0[:].rearrange("p c h j -> p (c h j)"),
-        )
+
+        for u in range(2):
+            round_pairs(0, raw0_scalar, u)
+        woven = []
+        for u in range(2):
+            round_pairs(1, raw0_vector, u)
+            part = stage.tile([P, 2 * P, 2, 2], BF16, name="woven%d" % u, align_bytes=64, offset=2048 * u)
+            nc.vector.tensor_copy(out=part[:], in_=pairs[u][:].rearrange("p h t m j -> p (t m) h j"))
+            woven.append(part)
+        for t0, part in zip((0, 2), woven):
+            nc.vector.quantize_mx(
+                out=w1_codes[0][:, t0 * P : (t0 + 2) * P].bitcast(FP8X4),
+                scales=w1_plane[0][:, t0 * P : (t0 + 2) * P],
+                in_=part[:].rearrange("p c h j -> p (c h j)"),
+            )
+        x_planes.append(early.tile([P, S], U8, name="x_plane1", align_bytes=64, offset=0))
+        nc.vector.memset(x_planes[1][:].bitcast(I32), 0)
+        warm = psum.tile([P, H], F32, name="warm", tag="bank%d" % (CHUNKS - 1))
+        for w in range(3):
+            nc.tensor.matmul_mx(
+                out=warm[:],
+                lhsT=w1_codes[0][:, 0:P].bitcast(FP8X4),
+                lhsT_scale=w1_plane[0][:, 0:P],
+                rhs=w1_codes[0][:].bitcast(FP8X4),
+                rhs_scale=w1_plane[0][:],
+                start=True,
+                stop=True,
+            )
         banks = [psum.tile([P, PACK, CHUNK], F32, name="bank%d" % b, tag="bank%d" % b) for b in range(2 * CHUNKS)]
         table1 = early.tile([P, T], U32, name="table1", align_bytes=64, offset=20480)
         load_words(1, table1)
         word_table.append(table1)
-        x_planes.append(early.tile([P, S], U8, name="x_plane1", align_bytes=64, offset=0))
-        nc.vector.memset(x_planes[1][:].bitcast(I32), 0)
         move_scale_rows(1)
 
         w2_plane = early.tile([P, N], U8, name="w2_plane", align_bytes=64, offset=12288)

@@ -94,7 +94,7 @@ def tile_picked_phpool_none_p_kernel(tc, x_words, x_scales, w1, w2_words, w2_sca
         word_table = [table0]
 
         w1_codes = [
-            early.tile([P, H], U32, name="w1_codes0", align_bytes=64, offset=1024),
+            early.tile([P, H], U32, name="w1_codes0", align_bytes=64, offset=S + N),
             keep.tile([P, H], U32, name="w1_codes1", align_bytes=64),
         ]
         w1_plane = [keep.tile([P, H], U8, name="w1_plane%d" % z, align_bytes=64) for z in range(PASSES)]
@@ -148,16 +148,24 @@ def tile_picked_phpool_none_p_kernel(tc, x_words, x_scales, w1, w2_words, w2_sca
         for u in range(2):
             round_pairs(1, raw0_vector, u)
             part = stage.tile([P, 2 * P, 2, 2], BF16, name="woven%d" % u, align_bytes=64, offset=2048 * u)
-            nc.vector.tensor_copy(out=part[:], in_=pairs[u][:].rearrange("p h t m j -> p (t m) h j"))
+            if u == 0:
+                nc.vector.tensor_copy(out=part[:], in_=pairs[u][:].rearrange("p h t m j -> p (t m) h j"))
+            else:
+                nc.scalar.copy(
+                    out=part[:].rearrange("p c h j -> p (c h j)").bitcast(U32).rearrange("p (c h) -> p c h", h=2),
+                    in_=pairs[u][:].rearrange("p h t m j -> p (h t m j)").bitcast(U32).rearrange("p (h c) -> p c h", h=2),
+                )
             woven.append(part)
+        late_planes = early.tile([P, S + N], U8, name="late_planes", align_bytes=64, offset=0)
+        nc.vector.memset(late_planes[:].bitcast(I32), 0)
         for t0, part in zip((0, 2), woven):
             nc.vector.quantize_mx(
                 out=w1_codes[0][:, t0 * P : (t0 + 2) * P].bitcast(FP8X4),
                 scales=w1_plane[0][:, t0 * P : (t0 + 2) * P],
                 in_=part[:].rearrange("p c h j -> p (c h j)"),
             )
-        x_planes.append(early.tile([P, S], U8, name="x_plane1", align_bytes=64, offset=0))
-        nc.vector.memset(x_planes[1][:].bitcast(I32), 0)
+        x_planes.append(late_planes[:, 0:S])
+        w2_plane = late_planes[:, S : S + N]
         warm = psum.tile([P, H], F32, name="warm", tag="bank%d" % (CHUNKS - 1))
         for w in range(3):
             nc.tensor.matmul_mx(
@@ -175,8 +183,6 @@ def tile_picked_phpool_none_p_kernel(tc, x_words, x_scales, w1, w2_words, w2_sca
         word_table.append(table1)
         move_scale_rows(1)
 
-        w2_plane = early.tile([P, N], U8, name="w2_plane", align_bytes=64, offset=12288)
-        nc.vector.memset(w2_plane[:].bitcast(I32), 0)
         for q in range(4):
             nc.sync.dma_start(
                 out=w2_plane[QUADRANT * q : QUADRANT * q + 4, :].bitcast(I32),

@@ -64,10 +64,8 @@ def tile_picked_phpool_none_p_kernel(tc, x_words, x_scales, w1, w2_words, w2_sca
         nc.vector.memset(zeros[0][:].bitcast(I32), 0)
         scale_table = keep.tile([P, T], U8, name="scale_table", align_bytes=64)
         nc.vector.memset(scale_table[:].bitcast(I32), 0)
-        nc.sync.dma_start(
-            out=scale_table[0:P:4, :].bitcast(I32),
-            in_=x_scales.rearrange("z q c -> q z c").bitcast(I32),
-        )
+        for z in range(PASSES):
+            nc.sync.dma_start(out=scale_table[4 + z : P : 8, :].bitcast(I32), in_=x_scales[z].bitcast(I32))
 
         x_planes = [keep.tile([P, S], U8, name="x_plane0", align_bytes=64)]
         nc.vector.tensor_copy(x_planes[0][:, 0:V].bitcast(I32), zeros[0][:].bitcast(I32))
@@ -86,7 +84,7 @@ def tile_picked_phpool_none_p_kernel(tc, x_words, x_scales, w1, w2_words, w2_sca
             for r in range(4):
                 nc.sync.dma_start(
                     out=x_planes[z][r:P:QUADRANT, :].bitcast(I32),
-                    in_=picked_scales[8 * r + 4 * z : P : QUADRANT, :].bitcast(I32),
+                    in_=picked_scales[8 * r + 4 + z : P : QUADRANT, :].bitcast(I32),
                 )
 
         move_scale_rows(0)
@@ -166,17 +164,6 @@ def tile_picked_phpool_none_p_kernel(tc, x_words, x_scales, w1, w2_words, w2_sca
             )
         x_planes.append(late_planes[:, 0:S])
         w2_plane = late_planes[:, S : S + N]
-        warm = psum.tile([P, H], F32, name="warm", tag="bank%d" % (CHUNKS - 1))
-        for w in range(3):
-            nc.tensor.matmul_mx(
-                out=warm[:],
-                lhsT=w1_codes[0][:, 0:P].bitcast(FP8X4),
-                lhsT_scale=w1_plane[0][:, 0:P],
-                rhs=w1_codes[0][:].bitcast(FP8X4),
-                rhs_scale=w1_plane[0][:],
-                start=True,
-                stop=True,
-            )
         banks = [psum.tile([P, PACK, CHUNK], F32, name="bank%d" % b, tag="bank%d" % b) for b in range(2 * CHUNKS)]
         table1 = early.tile([P, T], U32, name="table1", align_bytes=64, offset=20480)
         load_words(1, table1)
@@ -229,6 +216,8 @@ def tile_picked_phpool_none_p_kernel(tc, x_words, x_scales, w1, w2_words, w2_sca
         out_view = out.rearrange("(h p) v -> p h v", p=P)
         z_grouped = [keep.tile([P, CHUNK, PACK], BF16, name="z_grouped%d" % c, align_bytes=64) for c in range(CHUNKS)]
 
+        result = keep.tile([P, N // P, V], F32, name="result", align_bytes=64)
+
         def larger(c):
             nc.vector.tensor_tensor(
                 out=walk_words(z_grouped[c][:]) if c < CHUNKS - 1 else z_grouped[c][:],
@@ -263,13 +252,15 @@ def tile_picked_phpool_none_p_kernel(tc, x_words, x_scales, w1, w2_words, w2_sca
                     start=True,
                     stop=True,
                 )
-            result = keep.tile([P, N // P, CHUNK], F32, name="result%d" % c, align_bytes=64)
+            places = slice(c * CHUNK, (c + 1) * CHUNK)
             if last:
-                nc.scalar.copy(out=result[:, 0, :], in_=accs[0][:, 0, :])
-                nc.vector.tensor_copy(out=result[:, 1, :], in_=accs[1][:, 1, :])
+                nc.scalar.copy(out=result[:, 0, places], in_=accs[0][:, 0, :])
+                nc.vector.tensor_copy(out=result[:, 1, places], in_=accs[1][:, 1, :])
             else:
-                nc.scalar.copy(out=result[:], in_=accs[0][:])
-            nc.sync.dma_start(out=out_view[:, :, c * CHUNK : (c + 1) * CHUNK], in_=result[:])
+                nc.scalar.copy(out=result[:, :, places], in_=accs[0][:])
+            if c > 0:
+                stored = slice(0, 2 * CHUNK) if c == 1 else places
+                nc.sync.dma_start(out=out_view[:, :, stored], in_=result[:, :, stored])
 
         larger(0)
         for c in range(1, CHUNKS):

@@ -146,13 +146,10 @@ def tile_picked_phpool_none_p_kernel(tc, x_words, x_scales, w1, w2_words, w2_sca
         for u in range(2):
             round_pairs(1, raw0_vector, u)
             part = stage.tile([P, 2 * P, 2, 2], BF16, name="woven%d" % u, align_bytes=64, offset=2048 * u)
-            if u == 0:
-                nc.vector.tensor_copy(out=part[:], in_=pairs[u][:].rearrange("p h t m j -> p (t m) h j"))
-            else:
-                nc.scalar.copy(
-                    out=part[:].rearrange("p c h j -> p (c h j)").bitcast(U32).rearrange("p (c h) -> p c h", h=2),
-                    in_=pairs[u][:].rearrange("p h t m j -> p (h t m j)").bitcast(U32).rearrange("p (h c) -> p c h", h=2),
-                )
+            nc.scalar.copy(
+                out=part[:].rearrange("p c h j -> p (c h j)").bitcast(U32).rearrange("p (c h) -> p c h", h=2),
+                in_=pairs[u][:].rearrange("p h t m j -> p (h t m j)").bitcast(U32).rearrange("p (h c) -> p c h", h=2),
+            )
             woven.append(part)
         late_planes = early.tile([P, S + N], U8, name="late_planes", align_bytes=64, offset=0)
         nc.vector.memset(late_planes[:].bitcast(I32), 0)
@@ -165,6 +162,16 @@ def tile_picked_phpool_none_p_kernel(tc, x_words, x_scales, w1, w2_words, w2_sca
         x_planes.append(late_planes[:, 0:S])
         w2_plane = late_planes[:, S : S + N]
         banks = [psum.tile([P, PACK, CHUNK], F32, name="bank%d" % b, tag="bank%d" % b) for b in range(2 * CHUNKS)]
+        for b, width in enumerate((H, H // 2, H // 4)):
+            nc.tensor.matmul_mx(
+                out=banks[2 * CHUNKS - 1 - b][:].rearrange("p t c -> p (t c)")[:, 0:width],
+                lhsT=w1_codes[0][:, H - P : H].bitcast(FP8X4),
+                lhsT_scale=w1_plane[0][:, H - P : H],
+                rhs=w1_codes[0][:, 0:width].bitcast(FP8X4),
+                rhs_scale=w1_plane[0][:, 0:width],
+                start=True,
+                stop=True,
+            )
         table1 = early.tile([P, T], U32, name="table1", align_bytes=64, offset=20480)
         load_words(1, table1)
         word_table.append(table1)

@@ -101,8 +101,8 @@ def tile_picked_phpool_none_p_kernel(tc, x_words, x_scales, w1, w2_words, w2_sca
             grouped = stage.tile([P, PACK, P, PACK], BF16, name="w1_grouped%d" % z, align_bytes=64, offset=4096 * z)
             for copy, m0, m1, raw, first in parts:
                 copy(
-                    out=grouped[:, :, m0:m1, :].rearrange("p t m j -> p m t j"),
-                    in_=raw[:].rearrange("p j (m t) -> p m t j", t=PACK)[:, m0 - first : m1 - first],
+                    out=grouped[:, :, m0:m1, :].rearrange("p t m j -> p m j t"),
+                    in_=raw[:].rearrange("p j (m t) -> p m j t", t=PACK)[:, m0 - first : m1 - first],
                 )
             nc.vector.quantize_mx(
                 out=w1_codes[z][:].bitcast(FP8X4),

@@ -52,7 +52,7 @@ def tile_picked_phpool_none_p_kernel(tc, x_words, x_scales, w1, w2_words, w2_sca
             nc.sync.dma_start(out=raw[:], in_=rows[:, 2 * h : 2 * h + 2, :])
             return raw
 
-        raw0_scalar = load_row_pairs(0, 25600)
+        raw0_scalar = load_row_pairs(0, 28672)
 
         offsets = keep.tile([P, S // 16], U16, name="offsets")
         nc.sync.dma_start(offsets[:], offs)
@@ -62,15 +62,19 @@ def tile_picked_phpool_none_p_kernel(tc, x_words, x_scales, w1, w2_words, w2_sca
             for half, offset in enumerate((4096 - V // 2, 12288))
         ]
         nc.vector.memset(zeros[0][:].bitcast(I32), 0)
-        scale_table = keep.tile([P, T], U8, name="scale_table", align_bytes=64)
+        scale_table = early.tile([P, T], U8, name="scale_table", align_bytes=64, offset=20480)
         nc.vector.memset(scale_table[:].bitcast(I32), 0)
-        for z in range(PASSES):
-            nc.sync.dma_start(out=scale_table[4 + z : P : 8, :].bitcast(I32), in_=x_scales[z].bitcast(I32))
+        nc.sync.dma_start(
+            out=scale_table[0:P:4, :].bitcast(I32), in_=x_scales.rearrange("z q n -> q z n").bitcast(I32)
+        )
 
         x_planes = [keep.tile([P, S], U8, name="x_plane0", align_bytes=64)]
         nc.vector.tensor_copy(x_planes[0][:, 0:V].bitcast(I32), zeros[0][:].bitcast(I32))
         nc.vector.memset(zeros[1][:].bitcast(I32), 0)
         nc.vector.tensor_copy(x_planes[0][:, V:S].bitcast(I32), zeros[1][:].bitcast(I32))
+
+        late_planes = keep.tile([P, S + N], U8, name="late_planes", align_bytes=64)
+        nc.vector.memset(late_planes[:].bitcast(I32), 0)
 
         raw0_vector = load_row_pairs(1, 0)
         table0 = early.tile([P, T], U32, name="table0", align_bytes=64, offset=4096)
@@ -84,7 +88,7 @@ def tile_picked_phpool_none_p_kernel(tc, x_words, x_scales, w1, w2_words, w2_sca
             for r in range(4):
                 nc.sync.dma_start(
                     out=x_planes[z][r:P:QUADRANT, :].bitcast(I32),
-                    in_=picked_scales[8 * r + 4 + z : P : QUADRANT, :].bitcast(I32),
+                    in_=picked_scales[8 * r + 4 * z : P : QUADRANT, :].bitcast(I32),
                 )
 
         move_scale_rows(0)
@@ -151,8 +155,6 @@ def tile_picked_phpool_none_p_kernel(tc, x_words, x_scales, w1, w2_words, w2_sca
                 in_=pairs[u][:].rearrange("p h t m j -> p (h t m j)").bitcast(U32).rearrange("p (h c) -> p c h", h=2),
             )
             woven.append(part)
-        late_planes = early.tile([P, S + N], U8, name="late_planes", align_bytes=64, offset=0)
-        nc.vector.memset(late_planes[:].bitcast(I32), 0)
         for t0, part in zip((0, 2), woven):
             nc.vector.quantize_mx(
                 out=w1_codes[0][:, t0 * P : (t0 + 2) * P].bitcast(FP8X4),

@@ -64,9 +64,8 @@ def tile_picked_phpool_none_p_kernel(tc, x_words, x_scales, w1, w2_words, w2_sca
         nc.vector.memset(zeros[0][:].bitcast(I32), 0)
         scale_table = early.tile([P, T], U8, name="scale_table", align_bytes=64, offset=20480)
         nc.vector.memset(scale_table[:].bitcast(I32), 0)
-        nc.sync.dma_start(
-            out=scale_table[0:P:4, :].bitcast(I32), in_=x_scales.rearrange("z q n -> q z n").bitcast(I32)
-        )
+        for z in range(PASSES):
+            nc.sync.dma_start(out=scale_table[4 + z : P : 8, :].bitcast(I32), in_=x_scales[z].bitcast(I32))
 
         x_planes = [keep.tile([P, S], U8, name="x_plane0", align_bytes=64)]
         nc.vector.tensor_copy(x_planes[0][:, 0:V].bitcast(I32), zeros[0][:].bitcast(I32))
@@ -88,7 +87,7 @@ def tile_picked_phpool_none_p_kernel(tc, x_words, x_scales, w1, w2_words, w2_sca
             for r in range(4):
                 nc.sync.dma_start(
                     out=x_planes[z][r:P:QUADRANT, :].bitcast(I32),
-                    in_=picked_scales[8 * r + 4 * z : P : QUADRANT, :].bitcast(I32),
+                    in_=picked_scales[8 * r + 4 + z : P : QUADRANT, :].bitcast(I32),
                 )
 
         move_scale_rows(0)
@@ -101,18 +100,23 @@ def tile_picked_phpool_none_p_kernel(tc, x_words, x_scales, w1, w2_words, w2_sca
         ]
         w1_plane = [keep.tile([P, H], U8, name="w1_plane%d" % z, align_bytes=64) for z in range(PASSES)]
 
-        def quantize_w1(z, parts):
-            grouped = stage.tile([P, PACK, P, PACK], BF16, name="w1_grouped%d" % z, align_bytes=64, offset=4096 * z)
-            for copy, m0, m1, raw, first in parts:
-                copy(
-                    out=grouped[:, :, m0:m1, :].rearrange("p t m j -> p m j t"),
-                    in_=raw[:].rearrange("p j (m t) -> p m j t", t=PACK)[:, m0 - first : m1 - first],
+        def quantize_second_pass(raw):
+            halves = [
+                stage.tile([P, 2, P, PACK], BF16, name="w1_grouped%d" % u, align_bytes=64, offset=4096 + 2048 * u)
+                for u in range(2)
+            ]
+            for u in range(2):
+                for copy, m0, m1 in ((nc.scalar.copy, 0, SCALAR_M), (nc.vector.tensor_copy, SCALAR_M, P)):
+                    copy(
+                        out=halves[u][:, :, m0:m1, :].rearrange("p t m j -> p m j t"),
+                        in_=raw[:].rearrange("p j (m t) -> p m j t", t=PACK)[:, m0:m1, :, 2 * u : 2 * u + 2],
+                    )
+            for u in range(2):
+                nc.vector.quantize_mx(
+                    out=w1_codes[1][:, 2 * u * P : (2 * u + 2) * P].bitcast(FP8X4),
+                    scales=w1_plane[1][:, 2 * u * P : (2 * u + 2) * P],
+                    in_=halves[u][:].rearrange("p t m j -> p (t m j)"),
                 )
-            nc.vector.quantize_mx(
-                out=w1_codes[z][:].bitcast(FP8X4),
-                scales=w1_plane[z][:],
-                in_=grouped[:].rearrange("p t m j -> p (t m j)"),
-            )
 
         starts = [V, 0, V + SLICE, SLICE]
 
@@ -123,8 +127,8 @@ def tile_picked_phpool_none_p_kernel(tc, x_words, x_scales, w1, w2_words, w2_sca
             nc.vector.tensor_copy(picked[:], word_table[z][:].indirect(offsets[:, s0 // 16 : (s0 + SLICE) // 16]))
             return picked
 
-        def project(z, s0, picked):
-            for c0 in range(0, SLICE, CHUNK):
+        def project(z, s0, picked, columns, first_pass):
+            for c0 in columns:
                 for t in range(PACK):
                     nc.tensor.matmul_mx(
                         out=banks[(s0 + c0) // CHUNK][:, t, :],
@@ -132,8 +136,8 @@ def tile_picked_phpool_none_p_kernel(tc, x_words, x_scales, w1, w2_words, w2_sca
                         lhsT_scale=w1_plane[z][:, t * P : (t + 1) * P],
                         rhs=picked[:, c0 : c0 + CHUNK].bitcast(FP8X4),
                         rhs_scale=x_planes[z][:, s0 + c0 : s0 + c0 + CHUNK],
-                        start=(z == 0 and t == 0),
-                        stop=(z == PASSES - 1 and t == PACK - 1),
+                        start=(z == first_pass and t == 0),
+                        stop=(z != first_pass and t == PACK - 1),
                     )
 
         pairs = [keep.tile([P, 2, 2, P, 2], BF16, name="pairs%d" % u, align_bytes=64) for u in range(2)]
@@ -190,17 +194,17 @@ def tile_picked_phpool_none_p_kernel(tc, x_words, x_scales, w1, w2_words, w2_sca
             in_=w2_words[0].rearrange("p n t -> p (n t)").bitcast(I32),
         )
 
-        for s0 in starts:
-            project(0, s0, gather(0, s0))
-        quantize_w1(
-            1,
-            [
-                (nc.scalar.copy, 0, SCALAR_M, raw1, 0),
-                (nc.vector.tensor_copy, SCALAR_M, P, raw1, 0),
-            ],
-        )
-        for s0 in starts:
-            project(1, s0, gather(1, s0))
+        for s0 in starts[:-1]:
+            project(0, s0, gather(0, s0), (0, CHUNK), 0)
+        last_picked = gather(0, starts[-1])
+        project(0, starts[-1], last_picked, (0,), 0)
+        quantize_second_pass(raw1)
+        for s0 in starts[:-1]:
+            project(1, s0, gather(1, s0), (0, CHUNK), 0)
+        picked = gather(1, starts[-1])
+        project(1, starts[-1], picked, (0,), 0)
+        project(1, starts[-1], picked, (CHUNK,), 1)
+        project(0, starts[-1], last_picked, (CHUNK,), 1)
 
         def walk_bank(b):
             return banks[b][:].rearrange("p t (w i) -> p w t i", i=RUN)

@@ -168,11 +168,11 @@ def tile_picked_phpool_none_p_kernel(tc, x_words, x_scales, w1, w2_words, w2_sca
         x_planes.append(late_planes[:, 0:S])
         w2_plane = late_planes[:, S : S + N]
         banks = [psum.tile([P, PACK, CHUNK], F32, name="bank%d" % b, tag="bank%d" % b) for b in range(2 * CHUNKS)]
-        for b, width in enumerate((H, H // 2, H // 4)):
+        for b, width in enumerate((H, H, H)):
             nc.tensor.matmul_mx(
-                out=banks[2 * CHUNKS - 1 - b][:].rearrange("p t c -> p (t c)")[:, 0:width],
-                lhsT=w1_codes[0][:, H - P : H].bitcast(FP8X4),
-                lhsT_scale=w1_plane[0][:, H - P : H],
+                out=banks[b][0 : P // 2].rearrange("p t c -> p (t c)")[:, 0:width],
+                lhsT=w1_codes[0][:, H - P // 2 : H].bitcast(FP8X4),
+                lhsT_scale=w1_plane[0][:, H - P // 2 : H],
                 rhs=w1_codes[0][:, 0:width].bitcast(FP8X4),
                 rhs_scale=w1_plane[0][:, 0:width],
                 start=True,

@@ -168,16 +168,6 @@ def tile_picked_phpool_none_p_kernel(tc, x_words, x_scales, w1, w2_words, w2_sca
         x_planes.append(late_planes[:, 0:S])
         w2_plane = late_planes[:, S : S + N]
         banks = [psum.tile([P, PACK, CHUNK], F32, name="bank%d" % b, tag="bank%d" % b) for b in range(2 * CHUNKS)]
-        for b, width in enumerate((H, H, H)):
-            nc.tensor.matmul_mx(
-                out=banks[b][0 : P // 2].rearrange("p t c -> p (t c)")[:, 0:width],
-                lhsT=w1_codes[0][:, H - P // 2 : H].bitcast(FP8X4),
-                lhsT_scale=w1_plane[0][:, H - P // 2 : H],
-                rhs=w1_codes[0][:, 0:width].bitcast(FP8X4),
-                rhs_scale=w1_plane[0][:, 0:width],
-                start=True,
-                stop=True,
-            )
         table1 = early.tile([P, T], U32, name="table1", align_bytes=64, offset=20480)
         load_words(1, table1)
         word_table.append(table1)

from contextlib import ExitStack

import concourse.mybir as mybir

K, T, S, H, N, V = 1024, 2048, 1024, 512, 256, 512
FLOPS = 2 * K * H * S + 2 * H * N * V

F32 = mybir.dt.float32
BF16 = mybir.dt.bfloat16
I32 = mybir.dt.int32
U32 = mybir.dt.uint32
U16 = mybir.dt.uint16
U8 = mybir.dt.uint8
FP8X4 = mybir.dt.float8_e4m3fn_x4

P = 128
PACK = 4
K_PASS = P * PACK
PASSES = K // K_PASS
QUADRANT = 32
SLICE = 256
CHUNK = 128
CHUNKS = V // CHUNK
SCALAR_M = 72
RUN = 2


def tile_picked_phpool_none_p_kernel(tc, x_words, x_scales, w1, w2_words, w2_scales, offs, out):
    nc = tc.nc
    with ExitStack() as ctx:
        keep = ctx.enter_context(tc.tile_pool(name="keep", bufs=1))
        reuse = ctx.enter_context(tc.tile_pool(name="reuse", bufs=1))
        early = ctx.enter_context(tc.tile_pool(name="early", bufs=1))
        stage = ctx.enter_context(tc.tile_pool(name="stage", bufs=1))
        psum = ctx.enter_context(tc.psum_pool(name="psum", bufs=1))

        def load_words(z, table):
            nc.sync.dma_start(
                out=table[:].bitcast(I32),
                in_=x_words[z].rearrange("p n t -> p (n t)").bitcast(I32),
            )

        def load_w1(z, m0, m1, pool, offset):
            raw = pool.tile([P, PACK, PACK * (m1 - m0)], F32, name="raw%d_%d" % (z, m0), align_bytes=64, offset=offset)
            rows = w1[z * K_PASS : (z + 1) * K_PASS, PACK * m0 : PACK * m1]
            nc.sync.dma_start(out=raw[:], in_=rows.rearrange("(p j) c -> p j c", j=PACK))
            return raw

        def load_row_pairs(h, offset):
            raw = early.tile([P, 2, H], F32, name="raw0_pair%d" % h, align_bytes=64, offset=offset)
            rows = w1[0:K_PASS, :].rearrange("(p j) c -> p j c", j=PACK)
            nc.sync.dma_start(out=raw[:], in_=rows[:, 2 * h : 2 * h + 2, :])
            return raw

        raw0_scalar = load_row_pairs(0, 28672)

        offsets = keep.tile([P, S // 16], U16, name="offsets")
        nc.sync.dma_start(offsets[:], offs)

        zeros = [
            early.tile([P, V], U8, name="zeros%d" % half, align_bytes=64, offset=offset)
            for half, offset in enumerate((4096 - V // 2, 12288))
        ]
        nc.vector.memset(zeros[0][:].bitcast(I32), 0)
        scale_table = early.tile([P, T], U8, name="scale_table", align_bytes=64, offset=20480)
        nc.vector.memset(scale_table[:].bitcast(I32), 0)
        for z in range(PASSES):
            nc.sync.dma_start(out=scale_table[4 + z : P : 8, :].bitcast(I32), in_=x_scales[z].bitcast(I32))

        x_planes = [keep.tile([P, S], U8, name="x_plane0", align_bytes=64)]
        nc.vector.tensor_copy(x_planes[0][:, 0:V].bitcast(I32), zeros[0][:].bitcast(I32))
        nc.vector.memset(zeros[1][:].bitcast(I32), 0)
        nc.vector.tensor_copy(x_planes[0][:, V:S].bitcast(I32), zeros[1][:].bitcast(I32))

        late_planes = keep.tile([P, S + N], U8, name="late_planes", align_bytes=64)
        nc.vector.memset(late_planes[:].bitcast(I32), 0)

        raw0_vector = load_row_pairs(1, 0)
        table0 = early.tile([P, T], U32, name="table0", align_bytes=64, offset=4096)
        load_words(0, table0)
        raw1 = load_w1(1, 0, P, early, 12288)

        picked_scales = reuse.tile([P, S], U8, name="picked_scales", align_bytes=64, offset=0)
        nc.vector.tensor_copy(picked_scales[:], scale_table[:].indirect(offsets[:]))

        def move_scale_rows(z):
            for r in range(4):
                nc.sync.dma_start(
                    out=x_planes[z][r:P:QUADRANT, :].bitcast(I32),
                    in_=picked_scales[8 * r + 4 + z : P : QUADRANT, :].bitcast(I32),
                )

        move_scale_rows(0)

        word_table = [table0]

        w1_codes = [
            early.tile([P, H], U32, name="w1_codes0", align_bytes=64, offset=S + N),
            keep.tile([P, H], U32, name="w1_codes1", align_bytes=64),
        ]
        w1_plane = [keep.tile([P, H], U8, name="w1_plane%d" % z, align_bytes=64) for z in range(PASSES)]

        def quantize_second_pass(raw):
            halves = [
                stage.tile([P, 2, P, PACK], BF16, name="w1_grouped%d" % u, align_bytes=64, offset=4096 + 2048 * u)
                for u in range(2)
            ]
            for u in range(2):
                for copy, m0, m1 in ((nc.scalar.copy, 0, SCALAR_M), (nc.vector.tensor_copy, SCALAR_M, P)):
                    copy(
                        out=halves[u][:, :, m0:m1, :].rearrange("p t m j -> p m j t"),
                        in_=raw[:].rearrange("p j (m t) -> p m j t", t=PACK)[:, m0:m1, :, 2 * u : 2 * u + 2],
                    )
            for u in range(2):
                nc.vector.quantize_mx(
                    out=w1_codes[1][:, 2 * u * P : (2 * u + 2) * P].bitcast(FP8X4),
                    scales=w1_plane[1][:, 2 * u * P : (2 * u + 2) * P],
                    in_=halves[u][:].rearrange("p t m j -> p (t m j)"),
                )

        starts = [V, 0, V + SLICE, SLICE]

        def gather(z, s0):
            picked = stage.tile(
                [P, SLICE], U32, name="picked%d_%d" % (z, s0), align_bytes=64, offset=8192 + 4096 * z + 4 * s0
            )
            nc.vector.tensor_copy(picked[:], word_table[z][:].indirect(offsets[:, s0 // 16 : (s0 + SLICE) // 16]))
            return picked

        def project(z, s0, picked, columns, first_pass):
            for c0 in columns:
                for t in range(PACK):
                    nc.tensor.matmul_mx(
                        out=banks[(s0 + c0) // CHUNK][:, t, :],
                        lhsT=w1_codes[z][:, t * P : (t + 1) * P].bitcast(FP8X4),
                        lhsT_scale=w1_plane[z][:, t * P : (t + 1) * P],
                        rhs=picked[:, c0 : c0 + CHUNK].bitcast(FP8X4),
                        rhs_scale=x_planes[z][:, s0 + c0 : s0 + c0 + CHUNK],
                        start=(z == first_pass and t == 0),
                        stop=(z != first_pass and t == PACK - 1),
                    )

        pairs = [keep.tile([P, 2, 2, P, 2], BF16, name="pairs%d" % u, align_bytes=64) for u in range(2)]

        def round_pairs(h, raw, u):
            nc.scalar.copy(
                out=pairs[u][:, h].rearrange("p t m j -> p m t j"),
                in_=raw[:].rearrange("p j (m t) -> p m t j", t=PACK)[:, :, 2 * u : 2 * u + 2],
            )

        for u in range(2):
            round_pairs(0, raw0_scalar, u)
        woven = []
        for u in range(2):
            round_pairs(1, raw0_vector, u)
            part = stage.tile([P, 2 * P, 2, 2], BF16, name="woven%d" % u, align_bytes=64, offset=2048 * u)
            nc.scalar.copy(
                out=part[:].rearrange("p c h j -> p (c h j)").bitcast(U32).rearrange("p (c h) -> p c h", h=2),
                in_=pairs[u][:].rearrange("p h t m j -> p (h t m j)").bitcast(U32).rearrange("p (h c) -> p c h", h=2),
            )
            woven.append(part)
        for t0, part in zip((0, 2), woven):
            nc.vector.quantize_mx(
                out=w1_codes[0][:, t0 * P : (t0 + 2) * P].bitcast(FP8X4),
                scales=w1_plane[0][:, t0 * P : (t0 + 2) * P],
                in_=part[:].rearrange("p c h j -> p (c h j)"),
            )
        x_planes.append(late_planes[:, 0:S])
        w2_plane = late_planes[:, S : S + N]
        banks = [psum.tile([P, PACK, CHUNK], F32, name="bank%d" % b, tag="bank%d" % b) for b in range(2 * CHUNKS)]
        table1 = early.tile([P, T], U32, name="table1", align_bytes=64, offset=20480)
        load_words(1, table1)
        word_table.append(table1)
        move_scale_rows(1)

        for q in range(4):
            nc.sync.dma_start(
                out=w2_plane[QUADRANT * q : QUADRANT * q + 4, :].bitcast(I32),
                in_=w2_scales[0, 4 * q : 4 * q + 4, :].bitcast(I32),
            )
        w2_codes = early.tile([P, N], U32, name="w2_codes", align_bytes=64, offset=12288 + N)
        nc.sync.dma_start(
            out=w2_codes[:].bitcast(I32),
            in_=w2_words[0].rearrange("p n t -> p (n t)").bitcast(I32),
        )

        for s0 in starts[:-1]:
            project(0, s0, gather(0, s0), (0, CHUNK), 0)
        last_picked = gather(0, starts[-1])
        project(0, starts[-1], last_picked, (0,), 0)
        quantize_second_pass(raw1)
        for s0 in starts[:-1]:
            project(1, s0, gather(1, s0), (0, CHUNK), 0)
        picked = gather(1, starts[-1])
        project(1, starts[-1], picked, (0,), 0)
        project(1, starts[-1], picked, (CHUNK,), 1)
        project(0, starts[-1], last_picked, (CHUNK,), 1)

        def walk_bank(b):
            return banks[b][:].rearrange("p t (w i) -> p w t i", i=RUN)

        def walk_words(tile_ap):
            return tile_ap.rearrange("p (w i) t -> p w t i", i=RUN)

        def rounded_in_walk_order(b):
            values = keep.tile([P, CHUNK // RUN, PACK, RUN], BF16, name="rounded%d" % b, align_bytes=64)
            nc.scalar.copy(out=values[:], in_=walk_bank(b))
            return values[:]

        def rounded_in_word_order(b):
            values = keep.tile([P, CHUNK, PACK], BF16, name="rounded%d" % b, align_bytes=64)
            nc.scalar.copy(out=walk_words(values[:]), in_=walk_bank(b))
            return values[:]

        seconds = [rounded_in_walk_order(CHUNKS + c) for c in range(CHUNKS - 1)]
        seconds.append(rounded_in_word_order(2 * CHUNKS - 1))
        firsts = [walk_bank(c) for c in range(CHUNKS - 1)] + [rounded_in_word_order(CHUNKS - 1)]

        out_view = out.rearrange("(h p) v -> p h v", p=P)
        z_grouped = [keep.tile([P, CHUNK, PACK], BF16, name="z_grouped%d" % c, align_bytes=64) for c in range(CHUNKS)]

        result = keep.tile([P, N // P, V], F32, name="result", align_bytes=64)

        def larger(c):
            nc.vector.tensor_tensor(
                out=walk_words(z_grouped[c][:]) if c < CHUNKS - 1 else z_grouped[c][:],
                in0=firsts[c],
                in1=seconds[c],
                op=mybir.AluOpType.max,
            )

        def second_layer(c):
            if c < 2:
                z_codes = stage.tile(
                    [P, CHUNK], U32, name="z_codes%d" % c, align_bytes=64, offset=12288 + 4 * (V + SLICE, SLICE)[c]
                )
            else:
                z_codes = keep.tile([P, CHUNK], U32, name="z_codes%d" % c, align_bytes=64)
            z_plane = keep.tile([P, CHUNK], U8, name="z_plane%d" % c, align_bytes=64)
            nc.vector.quantize_mx(
                out=z_codes[:].bitcast(FP8X4), scales=z_plane[:], in_=z_grouped[c][:].rearrange("p v t -> p (v t)")
            )
            last = c == CHUNKS - 1
            accs = [
                psum.tile([P, N // P, CHUNK], F32, name="acc%d_%d" % (c, b), tag="bank%d" % (CHUNKS + c - CHUNKS * b))
                for b in range(2 if last else 1)
            ]
            for h in range(N // P):
                nc.tensor.matmul_mx(
                    out=accs[h if last else 0][:, h, :],
                    lhsT=w2_codes[:, h * P : (h + 1) * P].bitcast(FP8X4),
                    lhsT_scale=w2_plane[:, h * P : (h + 1) * P],
                    rhs=z_codes[:].bitcast(FP8X4),
                    rhs_scale=z_plane[:],
                    start=True,
                    stop=True,
                )
            places = slice(c * CHUNK, (c + 1) * CHUNK)
            if last:
                nc.scalar.copy(out=result[:, 0, places], in_=accs[0][:, 0, :])
                nc.vector.tensor_copy(out=result[:, 1, places], in_=accs[1][:, 1, :])
            else:
                nc.scalar.copy(out=result[:, :, places], in_=accs[0][:])
            if c > 0:
                stored = slice(0, 2 * CHUNK) if c == 1 else places
                nc.sync.dma_start(out=out_view[:, :, stored], in_=result[:, :, stored])

        larger(0)
        for c in range(1, CHUNKS):
            larger(c)
            second_layer(c - 1)
        second_layer(CHUNKS - 1)
